import numpy as np
import ml_dtypes


def mxq(x, axis, fmt="e4m3"):
    dtype, down = {"e4m3": (ml_dtypes.float8_e4m3fn, 7), "e5m2": (ml_dtypes.float8_e5m2, 14)}[fmt]
    v = np.moveaxis(np.asarray(x, np.float32).astype(ml_dtypes.bfloat16).astype(np.float64), axis, -1)
    blocks = v.reshape(v.shape[:-1] + (-1, 32))
    amax = np.abs(blocks).max(-1, keepdims=True)
    byte = np.maximum(np.where(amax > 0, np.frexp(amax)[1] - 1 + 127, 0) - down, 1)
    scale = np.exp2(byte - 127.0)
    codes = (blocks / scale).astype(np.float32).astype(dtype).astype(np.float64)
    return np.moveaxis((codes * scale).reshape(v.shape), -1, axis)


WIDE = False


def mx_kscale(k):
    if not WIDE:
        return np.ones(k)
    levels = np.array([10, -10, 5, -5, 0])
    if k % 512:
        return np.exp2(np.random.permutation(np.resize(levels, k // 32))).repeat(32)
    a = np.empty((k // 512, 16))
    for p in range(k // 512):
        a[p, :8] = np.random.permutation(np.resize(levels, 8))
        for g in range(8):
            far = levels[np.abs(levels - a[p, g]) >= 10]
            a[p, g + 8] = far[np.random.randint(len(far))]
    return np.exp2(a.ravel()).repeat(32)


def f64(x):
    return np.asarray(x).astype(np.float64)


def striped(idx):
    return np.tile(idx.reshape(-1, 16).T, (8, 1)).astype(np.uint16)


def unstriped(offs):
    return offs[:16].T.reshape(-1).astype(np.int64)


E2M1 = np.array([0.0, 0.5, 1.0, 1.5, 2.0, 3.0, 4.0, 6.0, -0.0, -0.5, -1.0, -1.5, -2.0, -3.0, -4.0, -6.0])


def pack_weight(w, fmt):
    k, n = w.shape
    w = f64(np.asarray(w, np.float32).astype(ml_dtypes.bfloat16)).reshape(k // 32, 32, n)
    amax = np.abs(w).max(1)
    if fmt == "e4m3":
        byte = np.frexp(amax)[1] - 1 + 127 - 7
    else:
        mant, ex = np.frexp(amax / 6.0)
        byte = np.where(mant > 0.5, ex, ex - 1) + 127
    byte = np.clip(np.where(amax > 0, byte, 1), 1, 254)
    scaled = (w * np.exp2(127.0 - byte)[:, None, :]).reshape(k, n).astype(np.float32)
    by_word = np.ascontiguousarray(scaled.reshape(k // 512, 128, 4, n).transpose(0, 1, 3, 2))
    if fmt == "e4m3":
        words = by_word.astype(ml_dtypes.float8_e4m3fn).view(np.uint8)
    else:
        c = by_word.astype(ml_dtypes.float4_e2m1fn).view(np.uint8) & 0xF
        words = (c[..., 0::2] | (c[..., 1::2] << 4)).reshape(k // 512, 128, 2 * n)
    return np.ascontiguousarray(words), np.ascontiguousarray(byte.astype(np.uint8).reshape(k // 512, 16, n))


def unpack_weight(words, scales, fmt):
    g, _, n = scales.shape
    words = np.ascontiguousarray(words).reshape(g, 128, n, -1)
    if fmt == "e4m3":
        vals = words.view(ml_dtypes.float8_e4m3fn).astype(np.float64)
    else:
        nib = np.empty((g, 128, n, 4), np.uint8)
        nib[..., 0::2] = words & 0xF
        nib[..., 1::2] = words >> 4
        vals = E2M1[nib]
    vals = vals * np.repeat(np.exp2(scales.astype(np.float64) - 127.0), 8, axis=1)[..., None]
    return vals.transpose(0, 1, 3, 2).reshape(g * 512, n)


def gelu(v):
    return 0.5 * v * (1.0 + np.tanh(np.sqrt(2.0 / np.pi) * (v + 0.044715 * v**3)))


K, H, N, T, TC, S, T2 = 1024, 1024, 256, 4096, 2048, 1024, 2048

def setup_inputs():
    n = np.random.standard_normal
    s = mx_kscale(K)[:, None]
    u = mx_kscale(H)[:, None]
    tab_words, tab_scales = pack_weight(n((K, T)) * s, "e4m3")
    tab2_words, tab2_scales = pack_weight(n((K, TC)) * s, "e4m3")
    w1_words, w1_scales = pack_weight(n((K, H)) / np.sqrt(K) / s, "e2m1")
    w2 = (n((K, H)) / np.sqrt(K) / s).astype(np.float32)
    w3_words, w3_scales = pack_weight(n((H, N)) / np.sqrt(H) / u, "e4m3")
    perm = np.random.permutation(T2)
    return {
        "tab_words": tab_words, "tab_scales": tab_scales,
        "tab2_words": tab2_words, "tab2_scales": tab2_scales,
        "offs": striped(np.random.permutation(T)[:S]),
        "offs2": striped(np.random.permutation(TC)[:S]),
        "offs3": striped(perm[:S]), "offs4": striped(perm[S:]),
        "w1_words": w1_words, "w1_scales": w1_scales, "w2": w2,
        "w3_words": w3_words, "w3_scales": w3_scales,
        "wg1": np.exp(0.3 * n((128, S))).astype(np.float32),
        "wg2": np.exp(0.3 * n((128, S))).astype(np.float32),
        "acc": (np.exp(0.3 * n((H, T2))) * u).astype(np.float32),
    }

def reference(tab_words, tab_scales, tab2_words, tab2_scales, offs, offs2, offs3, offs4,
              w1_words, w1_scales, w2, w3_words, w3_scales, wg1, wg2, acc):
    v = unpack_weight(tab_words, tab_scales, "e4m3")[:, unstriped(offs)]
    v2 = unpack_weight(tab2_words, tab2_scales, "e4m3")[:, unstriped(offs2)]
    a = unpack_weight(w1_words, w1_scales, "e2m1").T @ v
    h1 = np.log1p(np.square(a))
    b = mxq(f64(w2), 0, "e4m3").T @ v2
    h2 = b * np.exp(-0.2 * b)
    page = np.zeros((H, T2))
    page[:, unstriped(offs3)] = np.tile(f64(wg1), (H // 128, 1)) * h1
    page[:, unstriped(offs4)] = np.tile(f64(wg2), (H // 128, 1)) * h2
    z = page * f64(acc)
    return unpack_weight(w3_words, w3_scales, "e4m3").T @ mxq(z, 0, "e4m3")

@@ -1,0 +1,312 @@
+from contextlib import ExitStack
+
+import concourse.mybir as mybir
+
+K, H, N, T, TC, S, T2 = 1024, 1024, 256, 4096, 2048, 1024, 2048
+FLOPS = 2 * K * H * S * 2 + 2 * H * N * T2
+
+F32 = mybir.dt.float32
+BF16 = mybir.dt.bfloat16
+I32 = mybir.dt.int32
+U32 = mybir.dt.uint32
+U16 = mybir.dt.uint16
+U8 = mybir.dt.uint8
+FP8X4 = mybir.dt.float8_e4m3fn_x4
+FP4X4 = mybir.dt.float4_e2m1fn_x4
+ACT = mybir.ActivationFunctionType
+MULT = mybir.AluOpType.mult
+
+P = 128
+BANK = 512
+
+
+def tile_list_neutrino_tube_weave_kernel(
+    tc, tab_words, tab_scales, tab2_words, tab2_scales, offs, offs2, offs3, offs4,
+    w1_words, w1_scales, w2, w3_words, w3_scales, wg1, wg2, acc, out,
+):
+    nc = tc.nc
+    with ExitStack() as ctx:
+        lists = ctx.enter_context(tc.tile_pool(name="lists", bufs=1))
+        sb = ctx.enter_context(tc.tile_pool(name="sb", bufs=1))
+        psum = ctx.enter_context(tc.psum_pool(name="psum", bufs=1))
+
+        def tile(name, shape, dtype, tag=None):
+            return sb.tile(shape, dtype, name=name, tag=tag or name, align_bytes=64)
+
+        idx = [lists.tile([P, S // 16], U16, name="idx%d" % i) for i in range(4)]
+        banks = [psum.tile([P, BANK], F32, name="bank%d" % b) for b in range(8)]
+
+        tab_w = [tile("tab_w%d" % a, [P, T], I32, tag="wide%d" % a) for a in range(2)]
+        tab2_w = [tile("tab2_w%d" % a, [P, TC], I32, tag="page%d" % a) for a in range(2)]
+        tab_s = tile("tab_s", [P, 2 * T], U8)
+        tab2_s = tile("tab2_s", [P, TC], U8)
+        w1_raw = tile("w1_raw", [P, 2, H // 2], I32)
+        w1_s_raw = tile("w1_s_raw", [P, 2, H], U8)
+        w1_w = tile("w1_w", [P, 2, 2 * H], U8)
+        w1_s = tile("w1_s", [P, 2, H], U8)
+        w3_s = tile("w3_s", [P, N], U8)
+        v_w = [tile("v_w0", [P, S], U32, tag="tab_s"), tile("v_w1", [P, S], U32, tag="w1_s_raw")]
+        v2_w = [tile("v2_w0", [P, S], U32, tag="tab2_s"), tile("v2_w1", [P, S], U32)]
+        v_s = [tile("v_s%d" % a, [P, S], U8) for a in range(2)]
+        v2_s = tile("v2_s", [P, S], U8)
+        w2_w = [tile("w2_w%d" % g, [P, 2 * BANK], U32) for g in range(2)]
+        w2_s = [tile("w2_s%d" % g, [P, 2 * BANK], U8) for g in range(2)]
+        gain1 = tile("gain1", [P, 4 * S], F32)
+        gain2 = tile("gain2", [P, 4 * S], F32)
+        rows = [tile("rows%d" % i, [P, T2], F32) for i in range(2)]
+        h1 = [tile("h1_%d" % i, [P, S], F32) for i in range(4)]
+        h2 = [tile("h2_%d" % i, [P, S], F32) for i in range(4)]
+        woven = [tile("woven%d" % i, [P, 4096], BF16) for i in range(2)]
+        z_s = tile("z_s", [P, 2 * T2], U8)
+        one = tile("one", [P, 1], F32)
+        pages = [None] * 4
+
+        for plane in (tab_s[:], w1_s_raw[:].rearrange("p a c -> p (a c)"), tab2_s[:], w3_s[:]):
+            nc.vector.memset(plane.bitcast(I32), 0)
+        nc.vector.memset(one[:], 1.0)
+        zero = tile("zero", [P, 1], F32)
+        nc.scalar.activation(out=zero[:], in_=one[:], func=ACT.Ln)
+
+        def load_packed_scales(queue, plane, scales):
+            for q in range(4):
+                queue.dma_start(
+                    out=plane[32 * q : 32 * q + 8, :].bitcast(I32),
+                    in_=scales[:, 4 * q : 4 * q + 4, :].bitcast(I32),
+                )
+
+        def words(src):
+            return src.rearrange("p t i -> p (t i)").bitcast(I32)
+
+        def load_gain(dst, src, t0, t1):
+            view = src.rearrange("(m t) j -> m (t j)", t=4)
+            for q in range(4):
+                nc.sync.dma_start(out=dst[32 * q : 32 * q + 32, t0 * S : t1 * S], in_=view[:, t0 * S : t1 * S])
+
+        def load_scales(queue, plane, scales):
+            for q in range(4):
+                queue.dma_start(
+                    out=plane[32 * q : 32 * q + 4, :, :].bitcast(I32),
+                    in_=scales[:, 4 * q : 4 * q + 4, :].bitcast(I32).rearrange("a r c -> r a c"),
+                )
+
+        load_scales(nc.gpsimd, tab_s[:].rearrange("p (a c) -> p a c", a=2), tab_scales)
+        load_scales(nc.gpsimd, w1_s_raw[:], w1_scales)
+        load_packed_scales(nc.gpsimd, tab2_s, tab2_scales)
+        nc.sync.dma_start(idx[0][:], offs)
+        nc.sync.dma_start(out=w1_raw[:], in_=w1_words.bitcast(I32).rearrange("a p c -> p a c"))
+        for a in range(2):
+            nc.sync.dma_start(out=tab_w[a][:], in_=words(tab_words[a]))
+        nc.sync.dma_start(idx[1][:], offs2)
+        nc.sync.dma_start(idx[2][:], offs3)
+        load_gain(gain1, wg1, 0, 1)
+        for a in range(2):
+            nc.sync.dma_start(out=tab2_w[a][:], in_=words(tab2_words[a]))
+        load_gain(gain1, wg1, 1, 4)
+
+        def load_w2(g):
+            dst = tile("w2_raw%d" % g, [P, 2 * 2048], F32, tag="wide%d" % g)
+            for a in range(2):
+                nc.sync.dma_start(
+                    out=dst[:, 2048 * a : 2048 * (a + 1)].rearrange("p (j c) -> p j c", j=4),
+                    in_=w2[512 * a : 512 * (a + 1), 512 * g : 512 * (g + 1)].rearrange("(p j) c -> p j c", j=4),
+                )
+            return dst
+
+        def load_acc(s):
+            g, t = divmod(s, 4)
+            src = acc[512 * g : 512 * (g + 1), :].rearrange("(p t) m -> t p m", t=4)
+            nc.sync.dma_start(out=rows[s % 2][:], in_=src[t])
+
+
+        nc.vector.tensor_copy(
+            out=w1_w[:].rearrange("p a c -> p (a c)").bitcast(U16).rearrange("p (h t m) -> p h t m", h=4, t=4),
+            in_=w1_raw[:].rearrange("p a c -> p (a c)").bitcast(U16).rearrange("p (h m t) -> p h t m", h=4, t=4),
+        )
+        for a in range(2):
+            nc.vector.tensor_copy(v_s[a][:], tab_s[:, T * a : T * (a + 1)].indirect(idx[0][:]))
+        nc.vector.tensor_copy(v_w[0][:], tab_w[0][:].bitcast(U32).indirect(idx[0][:]))
+        nc.vector.tensor_copy(
+            out=w1_s[:].rearrange("p a (g t m) -> p (a g) t m", g=2, t=4),
+            in_=w1_s_raw[:].rearrange("p a (g m t) -> p (a g) t m", g=2, t=4),
+        )
+        nc.vector.tensor_copy(v_w[1][:], tab_w[1][:].bitcast(U32).indirect(idx[0][:]))
+        nc.vector.tensor_copy(v2_s[:], tab2_s[:].indirect(idx[1][:]))
+        for a in range(2):
+            nc.vector.tensor_copy(v2_w[a][:], tab2_w[a][:].bitcast(U32).indirect(idx[1][:]))
+
+        w2_raw = [load_w2(g) for g in range(2)]
+        for a in range(2):
+            pages[a] = tile("page%d" % a, [P, T2], F32)
+
+        def quantise_w2(g):
+            grouped = tile("w2_grouped%d" % g, [P, 4096], BF16, tag="page%d" % (2 + g))
+            for a in range(2):
+                nc.scalar.copy(
+                    out=grouped[:, 2048 * a : 2048 * (a + 1)].rearrange("p (t m j) -> p m t j", t=4, j=4),
+                    in_=w2_raw[g][:, 2048 * a : 2048 * (a + 1)].rearrange("p (j m t) -> p m t j", j=4, t=4),
+                )
+            nc.vector.quantize_mx(out=w2_w[g][:].bitcast(FP8X4), scales=w2_s[g][:], in_=grouped[:])
+            pages[2 + g] = tile("page%d" % (2 + g), [P, T2], F32)
+
+        turn = [0]
+
+        def next_banks():
+            turn[0] = turn[0] + 1
+            return banks[2 * (turn[0] % 2) : 2 * (turn[0] % 2) + 2]
+
+        def prepare1(s):
+            g, t = divmod(s, 4)
+            c0 = 512 * g + 128 * t
+            dst = h1[t]
+            for half, bank in enumerate(next_banks()):
+                cols = slice(BANK * half, BANK * (half + 1))
+                for a in range(2):
+                    nc.tensor.matmul_mx(
+                        out=bank[:],
+                        lhsT=w1_w[:, a, 2 * c0 : 2 * c0 + 256].bitcast(FP4X4),
+                        lhsT_scale=w1_s[:, a, c0 : c0 + 128],
+                        rhs=v_w[a][:, cols].bitcast(FP8X4),
+                        rhs_scale=v_s[a][:, cols],
+                        start=(a == 0), stop=(a == 1),
+                    )
+                nc.scalar.activation(out=dst[:, cols], in_=bank[:], func=ACT.Square, bias=zero[:])
+            nc.scalar.activation(out=dst[:], in_=dst[:], func=ACT.Ln, bias=one[:])
+            nc.gpsimd.tensor_tensor(out=dst[:], in0=dst[:], in1=gain1[:, t * S : (t + 1) * S], op=MULT)
+
+        def prepare2(s):
+            g, t = divmod(s, 4)
+            dst, b = h2[t], rows[s % 2][:, 0:S]
+            for half, bank in enumerate(next_banks()):
+                cols = slice(BANK * half, BANK * (half + 1))
+                for a in range(2):
+                    c0 = 512 * a + 128 * t
+                    nc.tensor.matmul_mx(
+                        out=bank[:],
+                        lhsT=w2_w[g][:, c0 : c0 + 128].bitcast(FP8X4),
+                        lhsT_scale=w2_s[g][:, c0 : c0 + 128],
+                        rhs=v2_w[a][:, cols].bitcast(FP8X4),
+                        rhs_scale=v2_s[4 * a : P, cols],
+                        start=(a == 0), stop=(a == 1),
+                    )
+                nc.scalar.copy(out=b[:, cols], in_=bank[:])
+                nc.scalar.activation(out=dst[:, cols], in_=bank[:], func=ACT.Exp, scale=-0.2)
+            nc.gpsimd.tensor_tensor(out=b, in0=b, in1=gain2[:, t * S : (t + 1) * S], op=MULT)
+            nc.gpsimd.tensor_tensor(out=dst[:], in0=dst[:], in1=b, op=MULT)
+
+        def scatter1(s):
+            nc.vector.tensor_copy(pages[s % 4][:].indirect(idx[2][:]), h1[s % 4][:])
+
+        def scatter2(s):
+            nc.vector.tensor_copy(pages[s % 4][:].indirect(idx[3][:]), h2[s % 4][:])
+
+        def accept(engine, s, c0, c1):
+            cols = slice(BANK * c0, BANK * c1)
+            engine.tensor_tensor(
+                out=planes[:, c0:c1, s % 4, :],
+                in0=pages[s % 4][:, cols].rearrange("p (c m) -> p c m", m=BANK),
+                in1=rows[s % 2][:, cols].rearrange("p (c m) -> p c m", m=BANK),
+                op=MULT,
+            )
+
+        def accept_slow(s):
+            accept(nc.gpsimd, s, 0, 2)
+            accept(nc.gpsimd, s, 2, 4)
+            if s % 4 < 2:
+                load_acc(s + 2)
+
+        def weave(copy, c):
+            dst = woven[c // 2][:, 2048 * (c % 2) : 2048 * (c % 2 + 1)]
+            copy(
+                out=dst.rearrange("p (c i t) -> p c t i", i=4, t=4),
+                in_=planes[:, c, :, :].rearrange("p t (c i) -> p c t i", i=4),
+            )
+
+        def quantise_z(g, c0, c1):
+            src = woven[c0 // 2][:, 2048 * (c0 % 2) : 2048 * (c0 % 2 + c1 - c0)]
+            cols = slice(T2 * g + BANK * c0, T2 * g + BANK * c1)
+            nc.vector.quantize_mx(out=z_w[:, cols].bitcast(FP8X4), scales=z_s[:, cols], in_=src)
+
+        def last_product(g, c):
+            cols = slice(T2 * g + BANK * c, T2 * g + BANK * (c + 1))
+            for n in range(2):
+                nc.tensor.matmul_mx(
+                    out=banks[(4 + 2 * c + n) % 8][:],
+                    lhsT=w3_w[:, g, 128 * n : 128 * (n + 1)].bitcast(FP8X4),
+                    lhsT_scale=w3_s[4 * g : P, 128 * n : 128 * (n + 1)],
+                    rhs=z_w[:, cols].bitcast(FP8X4),
+                    rhs_scale=z_s[:, cols],
+                    start=(g == 0), stop=(g == 1),
+                )
+
+        def store(c):
+            for n in range(2):
+                stage = h1[c][:, BANK * n : BANK * (n + 1)]
+                copy = nc.scalar.copy if n == 0 else nc.vector.tensor_copy
+                copy(out=stage, in_=banks[(4 + 2 * c + n) % 8][:])
+                queue = nc.scalar if n == 0 else nc.sync
+                queue.dma_start(out=out[128 * n : 128 * (n + 1), BANK * c : BANK * (c + 1)], in_=stage)
+
+        prepare1(0)
+        prepare1(1)
+        scatter1(0)
+        prepare1(2)
+        prepare1(3)
+        scatter1(1)
+        quantise_w2(0)
+        nc.sync.dma_start(idx[3][:], offs4)
+        load_gain(gain2, wg2, 0, 1)
+        quantise_w2(1)
+        planes = tile("planes", [P, 4, 4, BANK], BF16, tag="wide0")
+        z_w = tile("z_w", [P, 2 * T2], U32, tag="wide1")
+        load_gain(gain2, wg2, 1, 4)
+        load_packed_scales(nc.sync, w3_s, w3_scales)
+        prepare2(0)
+        scatter1(2)
+        prepare2(1)
+        scatter1(3)
+        prepare2(2)
+        load_acc(0)
+        scatter2(0)
+        prepare2(3)
+        load_acc(1)
+        accept_slow(0)
+        for t in range(1, 4):
+            scatter2(t)
+            prepare1(3 + t)
+            accept_slow(t)
+        scatter1(4)
+        prepare1(7)
+        scatter1(5)
+        prepare2(4)
+        weave(nc.scalar.copy, 0)
+        weave(nc.scalar.copy, 1)
+        scatter1(6)
+        prepare2(5)
+        weave(nc.scalar.copy, 2)
+        weave(nc.scalar.copy, 3)
+        scatter1(7)
+        quantise_z(0, 0, 2)
+        quantise_z(0, 2, 4)
+        prepare2(6)
+        load_acc(4)
+        scatter2(4)
+        prepare2(7)
+        w3_w = tile("w3_w", [P, 2, N], I32, tag="w2_w1")
+        nc.sync.dma_start(out=w3_w[:], in_=w3_words.rearrange("a p c i -> p a (c i)").bitcast(I32))
+        load_acc(5)
+        for c in range(4):
+            last_product(0, c)
+        accept_slow(4)
+        scatter2(5)
+        accept_slow(5)
+        scatter2(6)
+        accept_slow(6)
+        scatter2(7)
+        for c in range(4):
+            accept(nc.vector, 7, c, c + 1)
+        for c in range(4):
+            weave(nc.scalar.copy if c % 2 == 0 else nc.vector.tensor_copy, c)
+        for c in (0, 1, 3, 2):
+            quantise_z(1, c, c + 1)
+            last_product(1, c)
+            store(c)

@@ -54,12 +54,10 @@ def tile_list_neutrino_tube_weave_kernel(
         gain1 = tile("gain1", [P, 4 * S], F32)
         gain2 = tile("gain2", [P, 4 * S], F32)
         rows = [tile("rows%d" % i, [P, T2], F32) for i in range(2)]
-        h1 = [tile("h1_%d" % i, [P, S], F32) for i in range(4)]
+        h1 = [tile("h1_%d" % i, [P, S], F32) for i in range(8)]
         h2 = [tile("h2_%d" % i, [P, S], F32) for i in range(4)]
-        woven = [tile("woven%d" % i, [P, 4096], BF16) for i in range(2)]
-        z_s = tile("z_s", [P, 2 * T2], U8)
         one = tile("one", [P, 1], F32)
-        pages = [None] * 4
+        pages = [None] * 4 + [tile("page4", [P, T2], F32)]
 
         for plane in (tab_s[:], w1_s_raw[:].rearrange("p a c -> p (a c)"), tab2_s[:], w3_s[:]):
             nc.vector.memset(plane.bitcast(I32), 0)
@@ -157,7 +155,7 @@ def tile_list_neutrino_tube_weave_kernel(
         def prepare1(s):
             g, t = divmod(s, 4)
             c0 = 512 * g + 128 * t
-            dst = h1[t]
+            dst = h1[s]
             for half, bank in enumerate(next_banks()):
                 cols = slice(BANK * half, BANK * (half + 1))
                 for a in range(2):
@@ -194,16 +192,16 @@ def tile_list_neutrino_tube_weave_kernel(
             nc.gpsimd.tensor_tensor(out=dst[:], in0=dst[:], in1=b, op=MULT)
 
         def scatter1(s):
-            nc.vector.tensor_copy(pages[s % 4][:].indirect(idx[2][:]), h1[s % 4][:])
+            nc.vector.tensor_copy(pages[s % 5][:].indirect(idx[2][:]), h1[s][:])
 
         def scatter2(s):
-            nc.vector.tensor_copy(pages[s % 4][:].indirect(idx[3][:]), h2[s % 4][:])
+            nc.vector.tensor_copy(pages[s % 5][:].indirect(idx[3][:]), h2[s % 4][:])
 
         def accept(engine, s, c0, c1):
             cols = slice(BANK * c0, BANK * c1)
             engine.tensor_tensor(
-                out=planes[:, c0:c1, s % 4, :],
-                in0=pages[s % 4][:, cols].rearrange("p (c m) -> p c m", m=BANK),
+                out=planes[s // 4][:, c0:c1, s % 4, :],
+                in0=pages[s % 5][:, cols].rearrange("p (c m) -> p c m", m=BANK),
                 in1=rows[s % 2][:, cols].rearrange("p (c m) -> p c m", m=BANK),
                 op=MULT,
             )
@@ -214,15 +212,15 @@ def tile_list_neutrino_tube_weave_kernel(
             if s % 4 < 2:
                 load_acc(s + 2)
 
-        def weave(copy, c):
-            dst = woven[c // 2][:, 2048 * (c % 2) : 2048 * (c % 2 + 1)]
+        def weave(copy, g, c):
+            dst = woven[g][:, 2048 * c : 2048 * (c + 1)]
             copy(
                 out=dst.rearrange("p (c i t) -> p c t i", i=4, t=4),
-                in_=planes[:, c, :, :].rearrange("p t (c i) -> p c t i", i=4),
+                in_=planes[g][:, c, :, :].rearrange("p t (c i) -> p c t i", i=4),
             )
 
         def quantise_z(g, c0, c1):
-            src = woven[c0 // 2][:, 2048 * (c0 % 2) : 2048 * (c0 % 2 + c1 - c0)]
+            src = woven[g][:, 2048 * c0 : 2048 * c1]
             cols = slice(T2 * g + BANK * c0, T2 * g + BANK * c1)
             nc.vector.quantize_mx(out=z_w[:, cols].bitcast(FP8X4), scales=z_s[:, cols], in_=src)
 
@@ -252,14 +250,19 @@ def tile_list_neutrino_tube_weave_kernel(
         prepare1(2)
         prepare1(3)
         scatter1(1)
-        quantise_w2(0)
+        prepare1(4)
+        scatter1(4)
         nc.sync.dma_start(idx[3][:], offs4)
         load_gain(gain2, wg2, 0, 1)
+        quantise_w2(0)
         quantise_w2(1)
-        planes = tile("planes", [P, 4, 4, BANK], BF16, tag="wide0")
+        planes = [tile("planes0", [P, 4, 4, BANK], BF16, tag="wide0")]
+        woven = [tile("woven0", [P, 4 * T2], BF16, tag="wide2")]
         z_w = tile("z_w", [P, 2 * T2], U32, tag="wide1")
         load_gain(gain2, wg2, 1, 4)
         load_packed_scales(nc.sync, w3_s, w3_scales)
+        for s in range(5, 8):
+            prepare1(s)
         prepare2(0)
         scatter1(2)
         prepare2(1)
@@ -270,30 +273,31 @@ def tile_list_neutrino_tube_weave_kernel(
         prepare2(3)
         load_acc(1)
         accept_slow(0)
-        for t in range(1, 4):
-            scatter2(t)
-            prepare1(3 + t)
-            accept_slow(t)
-        scatter1(4)
-        prepare1(7)
-        scatter1(5)
+        scatter2(1)
+        accept_slow(1)
+        scatter2(2)
+        accept_slow(2)
+        scatter2(3)
         prepare2(4)
-        weave(nc.scalar.copy, 0)
-        weave(nc.scalar.copy, 1)
-        scatter1(6)
+        accept_slow(3)
+        for c in range(4):
+            weave(nc.scalar.copy, 0, c)
+        scatter1(5)
         prepare2(5)
-        weave(nc.scalar.copy, 2)
-        weave(nc.scalar.copy, 3)
-        scatter1(7)
-        quantise_z(0, 0, 2)
-        quantise_z(0, 2, 4)
+        scatter1(6)
         prepare2(6)
         load_acc(4)
-        scatter2(4)
+        scatter1(7)
         prepare2(7)
         w3_w = tile("w3_w", [P, 2, N], I32, tag="w2_w1")
         nc.sync.dma_start(out=w3_w[:], in_=w3_words.rearrange("a p c i -> p a (c i)").bitcast(I32))
         load_acc(5)
+        scatter2(4)
+        z_s = tile("z_s", [P, 2 * T2], U8, tag="h2_0")
+        quantise_z(0, 0, 2)
+        quantise_z(0, 2, 4)
+        planes.append(tile("planes1", [P, 4, 4, BANK], BF16, tag="wide2"))
+        woven.append(tile("woven1", [P, 4 * T2], BF16, tag="wide0"))
         for c in range(4):
             last_product(0, c)
         accept_slow(4)
@@ -305,7 +309,7 @@ def tile_list_neutrino_tube_weave_kernel(
         for c in range(4):
             accept(nc.vector, 7, c, c + 1)
         for c in range(4):
-            weave(nc.scalar.copy if c % 2 == 0 else nc.vector.tensor_copy, c)
+            weave(nc.scalar.copy if c % 2 == 0 else nc.vector.tensor_copy, 1, c)
         for c in (0, 1, 3, 2):
             quantise_z(1, c, c + 1)
             last_product(1, c)

@@ -28,6 +28,7 @@ def tile_list_neutrino_tube_weave_kernel(
     with ExitStack() as ctx:
         lists = ctx.enter_context(tc.tile_pool(name="lists", bufs=1))
         sb = ctx.enter_context(tc.tile_pool(name="sb", bufs=1))
+        shared = ctx.enter_context(tc.tile_pool(name="shared", bufs=1))
         psum = ctx.enter_context(tc.psum_pool(name="psum", bufs=1))
 
         def tile(name, shape, dtype, tag=None):
@@ -38,17 +39,17 @@ def tile_list_neutrino_tube_weave_kernel(
 
         tab_w = [tile("tab_w%d" % a, [P, T], I32, tag="wide%d" % a) for a in range(2)]
         tab2_w = [tile("tab2_w%d" % a, [P, TC], I32, tag="page%d" % a) for a in range(2)]
-        tab_s = tile("tab_s", [P, 2 * T], U8)
+        tab_s = shared.tile([P, T], U8, name="tab_s", align_bytes=64, offset=2 * S)
         tab2_s = tile("tab2_s", [P, TC], U8)
         w1_raw = tile("w1_raw", [P, 2, H // 2], I32)
         w1_s_raw = tile("w1_s_raw", [P, 2, H], U8)
-        w1_w = tile("w1_w", [P, 2, 2 * H], U8)
-        w1_s = tile("w1_s", [P, 2, H], U8)
+        w1_w = [tile("w1_w0", [P, 2, H], U8, tag="page2"), tile("w1_w1", [P, 2, H], U8)]
+        w1_s = [tile("w1_s0", [P, 2, BANK], U8, tag="page3"), tile("w1_s1", [P, 2, BANK], U8)]
         w3_s = tile("w3_s", [P, N], U8)
-        v_w = [tile("v_w0", [P, S], U32, tag="tab_s"), tile("v_w1", [P, S], U32, tag="w1_s_raw")]
-        v2_w = [tile("v2_w0", [P, S], U32, tag="tab2_s"), tile("v2_w1", [P, S], U32)]
+        v_w = [shared.tile([P, S], U32, name="v_w%d" % a, align_bytes=64, offset=4 * S * a) for a in range(2)]
+        v2_w = [tile("v2_w0", [P, S], U32), tile("v2_w1", [P, S], U32, tag="tab2_s")]
         v_s = [tile("v_s%d" % a, [P, S], U8) for a in range(2)]
-        v2_s = tile("v2_s", [P, S], U8)
+        v2_s = tile("v2_s", [P, S], U8, tag="w1_s_raw")
         w2_w = [tile("w2_w%d" % g, [P, 2 * BANK], U32) for g in range(2)]
         w2_s = [tile("w2_s%d" % g, [P, 2 * BANK], U8) for g in range(2)]
         gain1 = tile("gain1", [P, 4 * S], F32)
@@ -56,10 +57,11 @@ def tile_list_neutrino_tube_weave_kernel(
         rows = [tile("rows%d" % i, [P, T2], F32) for i in range(2)]
         h1 = [tile("h1_%d" % i, [P, S], F32) for i in range(8)]
         h2 = [tile("h2_%d" % i, [P, S], F32) for i in range(4)]
+        spare = [tile("spare%d" % i, [P, S], F32) for i in range(2)]
         one = tile("one", [P, 1], F32)
         pages = [None] * 4 + [tile("page4", [P, T2], F32)]
 
-        for plane in (tab_s[:], w1_s_raw[:].rearrange("p a c -> p (a c)"), tab2_s[:], w3_s[:]):
+        for plane in (tab_s[:], w1_s_raw[:].rearrange("p a c -> p (a c)"), tab2_s[:], v_s[1][:], w3_s[:]):
             nc.vector.memset(plane.bitcast(I32), 0)
         nc.vector.memset(one[:], 1.0)
         zero = tile("zero", [P, 1], F32)
@@ -87,18 +89,18 @@ def tile_list_neutrino_tube_weave_kernel(
                     in_=scales[:, 4 * q : 4 * q + 4, :].bitcast(I32).rearrange("a r c -> r a c"),
                 )
 
-        load_scales(nc.gpsimd, tab_s[:].rearrange("p (a c) -> p a c", a=2), tab_scales)
+        load_packed_scales(nc.gpsimd, tab_s, tab_scales)
         load_scales(nc.gpsimd, w1_s_raw[:], w1_scales)
         load_packed_scales(nc.gpsimd, tab2_s, tab2_scales)
         nc.sync.dma_start(idx[0][:], offs)
         nc.sync.dma_start(out=w1_raw[:], in_=w1_words.bitcast(I32).rearrange("a p c -> p a c"))
+        nc.sync.dma_start(idx[1][:], offs2)
+        nc.sync.dma_start(out=tab2_w[0][:], in_=words(tab2_words[0]))
         for a in range(2):
             nc.sync.dma_start(out=tab_w[a][:], in_=words(tab_words[a]))
-        nc.sync.dma_start(idx[1][:], offs2)
+        nc.sync.dma_start(out=tab2_w[1][:], in_=words(tab2_words[1]))
         nc.sync.dma_start(idx[2][:], offs3)
         load_gain(gain1, wg1, 0, 1)
-        for a in range(2):
-            nc.sync.dma_start(out=tab2_w[a][:], in_=words(tab2_words[a]))
         load_gain(gain1, wg1, 1, 4)
 
         def load_w2(g):
@@ -116,21 +118,23 @@ def tile_list_neutrino_tube_weave_kernel(
             nc.sync.dma_start(out=rows[s % 2][:], in_=src[t])
 
 
-        nc.vector.tensor_copy(
-            out=w1_w[:].rearrange("p a c -> p (a c)").bitcast(U16).rearrange("p (h t m) -> p h t m", h=4, t=4),
-            in_=w1_raw[:].rearrange("p a c -> p (a c)").bitcast(U16).rearrange("p (h m t) -> p h t m", h=4, t=4),
-        )
-        for a in range(2):
-            nc.vector.tensor_copy(v_s[a][:], tab_s[:, T * a : T * (a + 1)].indirect(idx[0][:]))
+        for g in range(2):
+            nc.vector.tensor_copy(
+                out=w1_w[g][:].bitcast(U16).rearrange("p a (t m) -> p a t m", t=4),
+                in_=w1_raw[:, :, 256 * g : 256 * (g + 1)].bitcast(U16).rearrange("p a (m t) -> p a t m", t=4),
+            )
+        nc.vector.tensor_copy(v2_w[0][:], tab2_w[0][:].bitcast(U32).indirect(idx[1][:]))
+        nc.vector.tensor_copy(v_s[0][:], tab_s[:].indirect(idx[0][:]))
+        nc.gpsimd.dma_start(out=v_s[1][0:112, :].bitcast(I32), in_=v_s[0][4:116, :].bitcast(I32))
         nc.vector.tensor_copy(v_w[0][:], tab_w[0][:].bitcast(U32).indirect(idx[0][:]))
-        nc.vector.tensor_copy(
-            out=w1_s[:].rearrange("p a (g t m) -> p (a g) t m", g=2, t=4),
-            in_=w1_s_raw[:].rearrange("p a (g m t) -> p (a g) t m", g=2, t=4),
-        )
+        for g in range(2):
+            nc.vector.tensor_copy(
+                out=w1_s[g][:].rearrange("p a (t m) -> p a t m", t=4),
+                in_=w1_s_raw[:, :, BANK * g : BANK * (g + 1)].rearrange("p a (m t) -> p a t m", t=4),
+            )
         nc.vector.tensor_copy(v_w[1][:], tab_w[1][:].bitcast(U32).indirect(idx[0][:]))
         nc.vector.tensor_copy(v2_s[:], tab2_s[:].indirect(idx[1][:]))
-        for a in range(2):
-            nc.vector.tensor_copy(v2_w[a][:], tab2_w[a][:].bitcast(U32).indirect(idx[1][:]))
+        nc.vector.tensor_copy(v2_w[1][:], tab2_w[1][:].bitcast(U32).indirect(idx[1][:]))
 
         w2_raw = [load_w2(g) for g in range(2)]
         for a in range(2):
@@ -152,29 +156,33 @@ def tile_list_neutrino_tube_weave_kernel(
             turn[0] = turn[0] + 1
             return banks[2 * (turn[0] % 2) : 2 * (turn[0] % 2) + 2]
 
-        def prepare1(s):
+        def prepare1(s, pieces=1):
             g, t = divmod(s, 4)
-            c0 = 512 * g + 128 * t
+            c0 = 128 * t
             dst = h1[s]
             for half, bank in enumerate(next_banks()):
                 cols = slice(BANK * half, BANK * (half + 1))
                 for a in range(2):
                     nc.tensor.matmul_mx(
                         out=bank[:],
-                        lhsT=w1_w[:, a, 2 * c0 : 2 * c0 + 256].bitcast(FP4X4),
-                        lhsT_scale=w1_s[:, a, c0 : c0 + 128],
+                        lhsT=w1_w[g][:, a, 2 * c0 : 2 * c0 + 256].bitcast(FP4X4),
+                        lhsT_scale=w1_s[g][:, a, c0 : c0 + 128],
                         rhs=v_w[a][:, cols].bitcast(FP8X4),
                         rhs_scale=v_s[a][:, cols],
                         start=(a == 0), stop=(a == 1),
                     )
                 nc.scalar.activation(out=dst[:, cols], in_=bank[:], func=ACT.Square, bias=zero[:])
-            nc.scalar.activation(out=dst[:], in_=dst[:], func=ACT.Ln, bias=one[:])
-            nc.gpsimd.tensor_tensor(out=dst[:], in0=dst[:], in1=gain1[:, t * S : (t + 1) * S], op=MULT)
+                if (half + 1) * pieces % 2 == 0:
+                    done = slice(BANK * (half + 1) - S // pieces, BANK * (half + 1))
+                    nc.scalar.activation(out=dst[:, done], in_=dst[:, done], func=ACT.Ln, bias=one[:])
+                    nc.gpsimd.tensor_tensor(
+                        out=dst[:, done], in0=dst[:, done], in1=gain1[:, t * S : (t + 1) * S][:, done], op=MULT
+                    )
 
-        def prepare2(s):
+        def respond2(s, b, pair):
             g, t = divmod(s, 4)
-            dst, b = h2[t], rows[s % 2][:, 0:S]
-            for half, bank in enumerate(next_banks()):
+            dst = h2[t]
+            for half, bank in enumerate(pair):
                 cols = slice(BANK * half, BANK * (half + 1))
                 for a in range(2):
                     c0 = 512 * a + 128 * t
@@ -186,13 +194,31 @@ def tile_list_neutrino_tube_weave_kernel(
                         rhs_scale=v2_s[4 * a : P, cols],
                         start=(a == 0), stop=(a == 1),
                     )
-                nc.scalar.copy(out=b[:, cols], in_=bank[:])
+                nc.scalar.copy(out=b[half], in_=bank[:])
                 nc.scalar.activation(out=dst[:, cols], in_=bank[:], func=ACT.Exp, scale=-0.2)
-            nc.gpsimd.tensor_tensor(out=b, in0=b, in1=gain2[:, t * S : (t + 1) * S], op=MULT)
-            nc.gpsimd.tensor_tensor(out=dst[:], in0=dst[:], in1=b, op=MULT)
 
-        def scatter1(s):
-            nc.vector.tensor_copy(pages[s % 5][:].indirect(idx[2][:]), h1[s][:])
+        def halves(b):
+            return [b[:, 0:BANK], b[:, BANK:S]]
+
+        def calibrate2(s, b, cols=slice(0, S)):
+            t = s % 4
+            nc.gpsimd.tensor_tensor(out=b, in0=b, in1=gain2[:, t * S : (t + 1) * S][:, cols], op=MULT)
+
+        def decay2(s, b, cols=slice(0, S)):
+            dst = h2[s % 4][:, cols]
+            nc.gpsimd.tensor_tensor(out=dst, in0=dst, in1=b, op=MULT)
+
+        def prepare2(s):
+            b = rows[s % 2][:, 0:S]
+            respond2(s, halves(b), next_banks())
+            calibrate2(s, b)
+            decay2(s, b)
+
+        def scatter1(s, pieces=1):
+            n = S // pieces
+            for i in range(pieces):
+                offsets = idx[2][:, i * n // 16 : (i + 1) * n // 16]
+                nc.vector.tensor_copy(pages[s % 5][:].indirect(offsets), h1[s][:, i * n : (i + 1) * n])
 
         def scatter2(s):
             nc.vector.tensor_copy(pages[s % 5][:].indirect(idx[3][:]), h2[s % 4][:])
@@ -244,9 +270,9 @@ def tile_list_neutrino_tube_weave_kernel(
                 queue = nc.scalar if n == 0 else nc.sync
                 queue.dma_start(out=out[128 * n : 128 * (n + 1), BANK * c : BANK * (c + 1)], in_=stage)
 
-        prepare1(0)
+        prepare1(0, pieces=2)
         prepare1(1)
-        scatter1(0)
+        scatter1(0, pieces=2)
         prepare1(2)
         prepare1(3)
         scatter1(1)
@@ -278,17 +304,25 @@ def tile_list_neutrino_tube_weave_kernel(
         scatter2(2)
         accept_slow(2)
         scatter2(3)
-        prepare2(4)
+        respond2(4, halves(rows[0]), banks[0:2])
         accept_slow(3)
+        calibrate2(4, rows[0][:, 0:S])
+        decay2(4, rows[0][:, 0:S])
         for c in range(4):
             weave(nc.scalar.copy, 0, c)
-        scatter1(5)
-        prepare2(5)
-        scatter1(6)
-        prepare2(6)
+        for s in (5, 6):
+            respond2(s, halves(spare[s % 2]), banks[0:2])
+        for step in (calibrate2, decay2):
+            for s in (5, 6):
+                step(s, spare[s % 2][:])
+        for s in (5, 6, 7):
+            scatter1(s)
+        last_b = [rows[half][:, 0:BANK] for half in range(2)]
+        respond2(7, last_b, banks[2:4])
+        for step in (calibrate2, decay2):
+            for half in range(2):
+                step(7, last_b[half], slice(BANK * half, BANK * (half + 1)))
         load_acc(4)
-        scatter1(7)
-        prepare2(7)
         w3_w = tile("w3_w", [P, 2, N], I32, tag="w2_w1")
         nc.sync.dma_start(out=w3_w[:], in_=w3_words.rearrange("a p c i -> p a (c i)").bitcast(I32))
         load_acc(5)

@@ -18,6 +18,7 @@ MULT = mybir.AluOpType.mult
 
 P = 128
 BANK = 512
+WIDE = 16384
 
 
 def tile_list_neutrino_tube_weave_kernel(
@@ -34,26 +35,28 @@ def tile_list_neutrino_tube_weave_kernel(
         def tile(name, shape, dtype, tag=None):
             return sb.tile(shape, dtype, name=name, tag=tag or name, align_bytes=64)
 
+        def wide_tile(name, shape, dtype, offset):
+            return shared.tile(shape, dtype, name=name, align_bytes=64, offset=offset)
+
         idx = [lists.tile([P, S // 16], U16, name="idx%d" % i) for i in range(4)]
         banks = [psum.tile([P, BANK], F32, name="bank%d" % b) for b in range(8)]
 
-        tab_w = [tile("tab_w%d" % a, [P, T], I32, tag="wide%d" % a) for a in range(2)]
+        seed = wide_tile("seed", [P, 32], F32, WIDE - 64)
+        tab_w = [wide_tile("tab_w%d" % a, [P, T], I32, WIDE * a) for a in range(2)]
+        w1_raw = tile("w1_raw", [P, 2, H // 2], I32, tag="page1")
         tab2_w = [tile("tab2_w%d" % a, [P, TC], I32, tag="page%d" % a) for a in range(2)]
-        tab_s = shared.tile([P, T], U8, name="tab_s", align_bytes=64, offset=2 * S)
-        tab2_s = tile("tab2_s", [P, TC], U8)
-        w1_raw = tile("w1_raw", [P, 2, H // 2], I32)
+        tab_s = tile("tab_s", [P, T], U8, tag="gain1")
+        tab2_s = tile("tab2_s", [P, TC], U8, tag="gain2")
         w1_s_raw = tile("w1_s_raw", [P, 2, H], U8)
         w1_w = [tile("w1_w0", [P, 2, H], U8, tag="page2"), tile("w1_w1", [P, 2, H], U8)]
         w1_s = [tile("w1_s0", [P, 2, BANK], U8, tag="page3"), tile("w1_s1", [P, 2, BANK], U8)]
         w3_s = tile("w3_s", [P, N], U8)
-        v_w = [shared.tile([P, S], U32, name="v_w%d" % a, align_bytes=64, offset=4 * S * a) for a in range(2)]
-        v2_w = [tile("v2_w0", [P, S], U32), tile("v2_w1", [P, S], U32, tag="tab2_s")]
+        v_w = [tile("v_w%d" % a, [P, S], U32) for a in range(2)]
+        v2_w = [tile("v2_w%d" % a, [P, S], U32) for a in range(2)]
         v_s = [tile("v_s%d" % a, [P, S], U8) for a in range(2)]
-        v2_s = tile("v2_s", [P, S], U8, tag="w1_s_raw")
+        v2_s = tile("v2_s", [P, S], U8)
         w2_w = [tile("w2_w%d" % g, [P, 2 * BANK], U32) for g in range(2)]
         w2_s = [tile("w2_s%d" % g, [P, 2 * BANK], U8) for g in range(2)]
-        gain1 = tile("gain1", [P, 4 * S], F32)
-        gain2 = tile("gain2", [P, 4 * S], F32)
         rows = [tile("rows%d" % i, [P, T2], F32) for i in range(2)]
         h1 = [tile("h1_%d" % i, [P, S], F32) for i in range(8)]
         h2 = [tile("h2_%d" % i, [P, S], F32) for i in range(4)]
@@ -61,11 +64,13 @@ def tile_list_neutrino_tube_weave_kernel(
         one = tile("one", [P, 1], F32)
         pages = [None] * 4 + [tile("page4", [P, T2], F32)]
 
-        for plane in (tab_s[:], w1_s_raw[:].rearrange("p a c -> p (a c)"), tab2_s[:], v_s[1][:], w3_s[:]):
+        zero = tile("zero", [P, 32], F32)
+        nc.vector.memset(tab_s[:].bitcast(I32), 0)
+        nc.vector.memset(seed[:], 1.0)
+        nc.scalar.activation(out=zero[:], in_=seed[:], func=ACT.Ln)
+        for plane in (w1_s_raw[:].rearrange("p a c -> p (a c)"), tab2_s[:], v_s[1][:], w3_s[:]):
             nc.vector.memset(plane.bitcast(I32), 0)
         nc.vector.memset(one[:], 1.0)
-        zero = tile("zero", [P, 1], F32)
-        nc.scalar.activation(out=zero[:], in_=one[:], func=ACT.Ln)
 
         def load_packed_scales(queue, plane, scales):
             for q in range(4):
@@ -89,22 +94,20 @@ def tile_list_neutrino_tube_weave_kernel(
                     in_=scales[:, 4 * q : 4 * q + 4, :].bitcast(I32).rearrange("a r c -> r a c"),
                 )
 
-        load_packed_scales(nc.gpsimd, tab_s, tab_scales)
-        load_scales(nc.gpsimd, w1_s_raw[:], w1_scales)
-        load_packed_scales(nc.gpsimd, tab2_s, tab2_scales)
         nc.sync.dma_start(idx[0][:], offs)
         nc.sync.dma_start(out=w1_raw[:], in_=w1_words.bitcast(I32).rearrange("a p c -> p a c"))
-        nc.sync.dma_start(idx[1][:], offs2)
+        load_packed_scales(nc.sync, tab_s, tab_scales)
+        for i, src in ((1, offs2), (2, offs3), (3, offs4)):
+            nc.sync.dma_start(idx[i][:], src)
         nc.sync.dma_start(out=tab2_w[0][:], in_=words(tab2_words[0]))
-        for a in range(2):
-            nc.sync.dma_start(out=tab_w[a][:], in_=words(tab_words[a]))
-        nc.sync.dma_start(out=tab2_w[1][:], in_=words(tab2_words[1]))
-        nc.sync.dma_start(idx[2][:], offs3)
-        load_gain(gain1, wg1, 0, 1)
-        load_gain(gain1, wg1, 1, 4)
+        nc.sync.dma_start(out=tab_w[0][:], in_=words(tab_words[0]))
+        load_scales(nc.sync, w1_s_raw[:], w1_scales)
+        nc.sync.dma_start(out=tab_w[1][:], in_=words(tab_words[1]))
+        load_packed_scales(nc.sync, tab2_s, tab2_scales)
+        load_packed_scales(nc.gpsimd, w3_s, w3_scales)
 
         def load_w2(g):
-            dst = tile("w2_raw%d" % g, [P, 2 * 2048], F32, tag="wide%d" % g)
+            dst = wide_tile("w2_raw%d" % g, [P, 2 * 2048], F32, WIDE * g)
             for a in range(2):
                 nc.sync.dma_start(
                     out=dst[:, 2048 * a : 2048 * (a + 1)].rearrange("p (j c) -> p j c", j=4),
@@ -123,9 +126,13 @@ def tile_list_neutrino_tube_weave_kernel(
                 out=w1_w[g][:].bitcast(U16).rearrange("p a (t m) -> p a t m", t=4),
                 in_=w1_raw[:, :, 256 * g : 256 * (g + 1)].bitcast(U16).rearrange("p a (m t) -> p a t m", t=4),
             )
+        nc.sync.dma_start(out=tab2_w[1][:], in_=words(tab2_words[1]))
         nc.vector.tensor_copy(v2_w[0][:], tab2_w[0][:].bitcast(U32).indirect(idx[1][:]))
         nc.vector.tensor_copy(v_s[0][:], tab_s[:].indirect(idx[0][:]))
         nc.gpsimd.dma_start(out=v_s[1][0:112, :].bitcast(I32), in_=v_s[0][4:116, :].bitcast(I32))
+        gain1 = tile("gain1", [P, 4 * S], F32)
+        load_gain(gain1, wg1, 0, 1)
+        load_gain(gain1, wg1, 1, 4)
         nc.vector.tensor_copy(v_w[0][:], tab_w[0][:].bitcast(U32).indirect(idx[0][:]))
         for g in range(2):
             nc.vector.tensor_copy(
@@ -171,7 +178,7 @@ def tile_list_neutrino_tube_weave_kernel(
                         rhs_scale=v_s[a][:, cols],
                         start=(a == 0), stop=(a == 1),
                     )
-                nc.scalar.activation(out=dst[:, cols], in_=bank[:], func=ACT.Square, bias=zero[:])
+                nc.scalar.activation(out=dst[:, cols], in_=bank[:], func=ACT.Square, bias=zero[:, 0:1])
                 if (half + 1) * pieces % 2 == 0:
                     done = slice(BANK * (half + 1) - S // pieces, BANK * (half + 1))
                     nc.scalar.activation(out=dst[:, done], in_=dst[:, done], func=ACT.Ln, bias=one[:])
@@ -278,15 +285,13 @@ def tile_list_neutrino_tube_weave_kernel(
         scatter1(1)
         prepare1(4)
         scatter1(4)
-        nc.sync.dma_start(idx[3][:], offs4)
-        load_gain(gain2, wg2, 0, 1)
+        gain2 = tile("gain2", [P, 4 * S], F32)
+        load_gain(gain2, wg2, 0, 4)
         quantise_w2(0)
         quantise_w2(1)
-        planes = [tile("planes0", [P, 4, 4, BANK], BF16, tag="wide0")]
+        planes = [wide_tile("planes0", [P, 4, 4, BANK], BF16, 0)]
         woven = [tile("woven0", [P, 4 * T2], BF16, tag="wide2")]
-        z_w = tile("z_w", [P, 2 * T2], U32, tag="wide1")
-        load_gain(gain2, wg2, 1, 4)
-        load_packed_scales(nc.sync, w3_s, w3_scales)
+        z_w = wide_tile("z_w", [P, 2 * T2], U32, WIDE)
         for s in range(5, 8):
             prepare1(s)
         prepare2(0)
@@ -331,7 +336,7 @@ def tile_list_neutrino_tube_weave_kernel(
         quantise_z(0, 0, 2)
         quantise_z(0, 2, 4)
         planes.append(tile("planes1", [P, 4, 4, BANK], BF16, tag="wide2"))
-        woven.append(tile("woven1", [P, 4 * T2], BF16, tag="wide0"))
+        woven.append(wide_tile("woven1", [P, 4 * T2], BF16, 0))
         for c in range(4):
             last_product(0, c)
         accept_slow(4)

@@ -17,8 +17,13 @@ ACT = mybir.ActivationFunctionType
 MULT = mybir.AluOpType.mult
 
 P = 128
+PACK = 4
+PASS = P * PACK
 BANK = 512
-WIDE = 16384
+CHUNKS = T2 // BANK
+SLICES = H // P
+PAGES = 5
+REGION = 4 * T
 
 
 def tile_list_neutrino_tube_weave_kernel(
@@ -35,63 +40,59 @@ def tile_list_neutrino_tube_weave_kernel(
         def tile(name, shape, dtype, tag=None):
             return sb.tile(shape, dtype, name=name, tag=tag or name, align_bytes=64)
 
-        def wide_tile(name, shape, dtype, offset):
-            return shared.tile(shape, dtype, name=name, align_bytes=64, offset=offset)
+        def placed(name, shape, dtype, offset, align=64):
+            return shared.tile(shape, dtype, name=name, align_bytes=align, offset=offset)
 
         idx = [lists.tile([P, S // 16], U16, name="idx%d" % i) for i in range(4)]
         banks = [psum.tile([P, BANK], F32, name="bank%d" % b) for b in range(8)]
 
-        seed = wide_tile("seed", [P, 32], F32, WIDE - 64)
-        tab_w = [wide_tile("tab_w%d" % a, [P, T], I32, WIDE * a) for a in range(2)]
+        seed = placed("seed", [P, 2 * SLICES], F32, REGION - 32, align=32)
+        tab_w = [placed("tab_w%d" % a, [P, T], I32, REGION * a) for a in range(2)]
+        across_pages = 2 * REGION + REGION // 4
         w1_raw = tile("w1_raw", [P, 2, H // 2], I32, tag="page1")
         tab2_w = [tile("tab2_w%d" % a, [P, TC], I32, tag="page%d" % a) for a in range(2)]
         tab_s = tile("tab_s", [P, T], U8, tag="gain1")
         tab2_s = tile("tab2_s", [P, TC], U8, tag="gain2")
         w1_s_raw = tile("w1_s_raw", [P, 2, H], U8)
-        w1_w = [tile("w1_w0", [P, 2, H], U8, tag="page2"), tile("w1_w1", [P, 2, H], U8)]
-        w1_s = [tile("w1_s0", [P, 2, BANK], U8, tag="page3"), tile("w1_s1", [P, 2, BANK], U8)]
+        w1_w = [tile("w1_w0", [P, 2, H], U8), placed("w1_w1", [P, 2, H], U8, across_pages)]
+        w1_s = [tile("w1_s0", [P, 2, PASS], U8), tile("w1_s1", [P, 2, PASS], U8, tag="w2_bf16_1")]
         w3_s = tile("w3_s", [P, N], U8)
         v_w = [tile("v_w%d" % a, [P, S], U32) for a in range(2)]
         v2_w = [tile("v2_w%d" % a, [P, S], U32) for a in range(2)]
         v_s = [tile("v_s%d" % a, [P, S], U8) for a in range(2)]
         v2_s = tile("v2_s", [P, S], U8)
-        w2_w = [tile("w2_w%d" % g, [P, 2 * BANK], U32) for g in range(2)]
-        w2_s = [tile("w2_s%d" % g, [P, 2 * BANK], U8) for g in range(2)]
+        w2_w = [None, tile("w2_w1", [P, 2 * PASS], U32)]
+        w2_s = [tile("w2_s%d" % g, [P, 2 * PASS], U8) for g in range(2)]
         rows = [tile("rows%d" % i, [P, T2], F32) for i in range(2)]
-        h1 = [tile("h1_%d" % i, [P, S], F32) for i in range(8)]
-        h2 = [tile("h2_%d" % i, [P, S], F32) for i in range(4)]
-        spare = [tile("spare%d" % i, [P, S], F32) for i in range(2)]
+        h1 = [tile("h1_%d" % s, [P, S], F32) for s in range(SLICES)]
+        h2 = [tile("h2_%d" % t, [P, S], F32) for t in range(PACK)]
+        spare_b = [tile("spare_b%d" % i, [P, S], F32) for i in range(2)]
         one = tile("one", [P, 1], F32)
-        pages = [None] * 4 + [tile("page4", [P, T2], F32)]
+        pages = [None] * (PAGES - 1) + [tile("page4", [P, T2], F32)]
 
-        zero = tile("zero", [P, 32], F32)
+        zero = tile("zero", [P, 2 * SLICES], F32)
         nc.vector.memset(tab_s[:].bitcast(I32), 0)
         nc.vector.memset(seed[:], 1.0)
         nc.scalar.activation(out=zero[:], in_=seed[:], func=ACT.Ln)
-        for plane in (w1_s_raw[:].rearrange("p a c -> p (a c)"), tab2_s[:], v_s[1][:], w3_s[:]):
-            nc.vector.memset(plane.bitcast(I32), 0)
+        for cleared in (w1_s_raw[:].rearrange("p a c -> p (a c)"), tab2_s[:], v_s[1][:], w3_s[:]):
+            nc.vector.memset(cleared.bitcast(I32), 0)
         nc.vector.memset(one[:], 1.0)
 
-        def load_packed_scales(queue, plane, scales):
-            for q in range(4):
+        def load_packed_scales(queue, dst, scales):
+            for quad in range(4):
                 queue.dma_start(
-                    out=plane[32 * q : 32 * q + 8, :].bitcast(I32),
-                    in_=scales[:, 4 * q : 4 * q + 4, :].bitcast(I32),
+                    out=dst[32 * quad : 32 * quad + 8, :].bitcast(I32),
+                    in_=scales[:, 4 * quad : 4 * quad + 4, :].bitcast(I32),
                 )
 
         def words(src):
             return src.rearrange("p t i -> p (t i)").bitcast(I32)
 
-        def load_gain(dst, src, t0, t1):
-            view = src.rearrange("(m t) j -> m (t j)", t=4)
-            for q in range(4):
-                nc.sync.dma_start(out=dst[32 * q : 32 * q + 32, t0 * S : t1 * S], in_=view[:, t0 * S : t1 * S])
-
-        def load_scales(queue, plane, scales):
-            for q in range(4):
-                queue.dma_start(
-                    out=plane[32 * q : 32 * q + 4, :, :].bitcast(I32),
-                    in_=scales[:, 4 * q : 4 * q + 4, :].bitcast(I32).rearrange("a r c -> r a c"),
+        def load_gain(dst, wg, t0, t1):
+            view = wg.rearrange("(m t) j -> m (t j)", t=PACK)
+            for quad in (0, 2, 1, 3):
+                nc.sync.dma_start(
+                    out=dst[32 * quad : 32 * quad + 32, t0 * S : t1 * S], in_=view[:, t0 * S : t1 * S]
                 )
 
         nc.sync.dma_start(idx[0][:], offs)
@@ -101,43 +102,46 @@ def tile_list_neutrino_tube_weave_kernel(
             nc.sync.dma_start(idx[i][:], src)
         nc.sync.dma_start(out=tab2_w[0][:], in_=words(tab2_words[0]))
         nc.sync.dma_start(out=tab_w[0][:], in_=words(tab_words[0]))
-        load_scales(nc.sync, w1_s_raw[:], w1_scales)
+        for quad in range(4):
+            nc.sync.dma_start(
+                out=w1_s_raw[32 * quad : 32 * quad + 4, :, :].bitcast(I32),
+                in_=w1_scales[:, 4 * quad : 4 * quad + 4, :].bitcast(I32).rearrange("a r c -> r a c"),
+            )
         nc.sync.dma_start(out=tab_w[1][:], in_=words(tab_words[1]))
         load_packed_scales(nc.sync, tab2_s, tab2_scales)
         load_packed_scales(nc.gpsimd, w3_s, w3_scales)
 
         def load_w2(g):
-            dst = wide_tile("w2_raw%d" % g, [P, 2 * 2048], F32, WIDE * g)
+            dst = placed("w2_raw%d" % g, [P, 2 * PACK * PASS], F32, REGION * g)
             for a in range(2):
                 nc.sync.dma_start(
-                    out=dst[:, 2048 * a : 2048 * (a + 1)].rearrange("p (j c) -> p j c", j=4),
-                    in_=w2[512 * a : 512 * (a + 1), 512 * g : 512 * (g + 1)].rearrange("(p j) c -> p j c", j=4),
+                    out=dst[:, PACK * PASS * a : PACK * PASS * (a + 1)].rearrange("p (j c) -> p j c", j=PACK),
+                    in_=w2[PASS * a : PASS * (a + 1), PASS * g : PASS * (g + 1)].rearrange("(p j) c -> p j c", j=PACK),
                 )
             return dst
 
         def load_acc(s):
-            g, t = divmod(s, 4)
-            src = acc[512 * g : 512 * (g + 1), :].rearrange("(p t) m -> t p m", t=4)
+            g, t = divmod(s, PACK)
+            src = acc[PASS * g : PASS * (g + 1), :].rearrange("(p t) m -> t p m", t=PACK)
             nc.sync.dma_start(out=rows[s % 2][:], in_=src[t])
-
 
         for g in range(2):
             nc.vector.tensor_copy(
-                out=w1_w[g][:].bitcast(U16).rearrange("p a (t m) -> p a t m", t=4),
-                in_=w1_raw[:, :, 256 * g : 256 * (g + 1)].bitcast(U16).rearrange("p a (m t) -> p a t m", t=4),
+                out=w1_w[g][:].bitcast(U16).rearrange("p a (t m) -> p a t m", t=PACK),
+                in_=w1_raw[:, :, PASS // 2 * g : PASS // 2 * (g + 1)].bitcast(U16).rearrange("p a (m t) -> p a t m", t=PACK),
             )
         nc.sync.dma_start(out=tab2_w[1][:], in_=words(tab2_words[1]))
         nc.vector.tensor_copy(v2_w[0][:], tab2_w[0][:].bitcast(U32).indirect(idx[1][:]))
         nc.vector.tensor_copy(v_s[0][:], tab_s[:].indirect(idx[0][:]))
         nc.gpsimd.dma_start(out=v_s[1][0:112, :].bitcast(I32), in_=v_s[0][4:116, :].bitcast(I32))
-        gain1 = tile("gain1", [P, 4 * S], F32)
-        load_gain(gain1, wg1, 0, 1)
-        load_gain(gain1, wg1, 1, 4)
+        gain1 = tile("gain1", [P, PACK * S], F32)
+        for t0, t1 in ((0, 1), (1, 2), (2, 4)):
+            load_gain(gain1, wg1, t0, t1)
         nc.vector.tensor_copy(v_w[0][:], tab_w[0][:].bitcast(U32).indirect(idx[0][:]))
         for g in range(2):
             nc.vector.tensor_copy(
-                out=w1_s[g][:].rearrange("p a (t m) -> p a t m", t=4),
-                in_=w1_s_raw[:, :, BANK * g : BANK * (g + 1)].rearrange("p a (m t) -> p a t m", t=4),
+                out=w1_s[g][:].rearrange("p a (t m) -> p a t m", t=PACK),
+                in_=w1_s_raw[:, :, PASS * g : PASS * (g + 1)].rearrange("p a (m t) -> p a t m", t=PACK),
             )
         nc.vector.tensor_copy(v_w[1][:], tab_w[1][:].bitcast(U32).indirect(idx[0][:]))
         nc.vector.tensor_copy(v2_s[:], tab2_s[:].indirect(idx[1][:]))
@@ -147,77 +151,72 @@ def tile_list_neutrino_tube_weave_kernel(
         for a in range(2):
             pages[a] = tile("page%d" % a, [P, T2], F32)
 
-        def quantise_w2(g):
-            grouped = tile("w2_grouped%d" % g, [P, 4096], BF16, tag="page%d" % (2 + g))
+        def quantise_w2(g, rounded):
             for a in range(2):
+                cols = slice(PACK * PASS * a, PACK * PASS * (a + 1))
                 nc.scalar.copy(
-                    out=grouped[:, 2048 * a : 2048 * (a + 1)].rearrange("p (t m j) -> p m t j", t=4, j=4),
-                    in_=w2_raw[g][:, 2048 * a : 2048 * (a + 1)].rearrange("p (j m t) -> p m t j", j=4, t=4),
+                    out=rounded[:, cols].rearrange("p (t m j) -> p m t j", t=PACK, j=PACK),
+                    in_=w2_raw[g][:, cols].rearrange("p (j m t) -> p m t j", j=PACK, t=PACK),
                 )
-            nc.vector.quantize_mx(out=w2_w[g][:].bitcast(FP8X4), scales=w2_s[g][:], in_=grouped[:])
-            pages[2 + g] = tile("page%d" % (2 + g), [P, T2], F32)
+            nc.vector.quantize_mx(out=w2_w[g][:].bitcast(FP8X4), scales=w2_s[g][:], in_=rounded[:])
 
-        turn = [0]
+        bank_pairs = [banks[0:2], banks[2:4]]
 
-        def next_banks():
-            turn[0] = turn[0] + 1
-            return banks[2 * (turn[0] % 2) : 2 * (turn[0] % 2) + 2]
-
-        def prepare1(s, pieces=1):
-            g, t = divmod(s, 4)
-            c0 = 128 * t
-            dst = h1[s]
-            for half, bank in enumerate(next_banks()):
+        def make_h1(s, pieces=1):
+            g, t = divmod(s, PACK)
+            for half, bank in enumerate(bank_pairs[(s + 1) % 2]):
                 cols = slice(BANK * half, BANK * (half + 1))
                 for a in range(2):
                     nc.tensor.matmul_mx(
                         out=bank[:],
-                        lhsT=w1_w[g][:, a, 2 * c0 : 2 * c0 + 256].bitcast(FP4X4),
-                        lhsT_scale=w1_s[g][:, a, c0 : c0 + 128],
+                        lhsT=w1_w[g][:, a, 2 * P * t : 2 * P * (t + 1)].bitcast(FP4X4),
+                        lhsT_scale=w1_s[g][:, a, P * t : P * (t + 1)],
                         rhs=v_w[a][:, cols].bitcast(FP8X4),
                         rhs_scale=v_s[a][:, cols],
                         start=(a == 0), stop=(a == 1),
                     )
-                nc.scalar.activation(out=dst[:, cols], in_=bank[:], func=ACT.Square, bias=zero[:, 0:1])
-                if (half + 1) * pieces % 2 == 0:
-                    done = slice(BANK * (half + 1) - S // pieces, BANK * (half + 1))
-                    nc.scalar.activation(out=dst[:, done], in_=dst[:, done], func=ACT.Ln, bias=one[:])
+                column = 2 * s + half
+                nc.scalar.activation(
+                    out=h1[s][:, cols], in_=bank[:], func=ACT.Square, bias=zero[:, column : column + 1]
+                )
+                if pieces == 2 or half == 1:
+                    done = cols if pieces == 2 else slice(0, S)
+                    nc.scalar.activation(out=h1[s][:, done], in_=h1[s][:, done], func=ACT.Ln, bias=one[:])
                     nc.gpsimd.tensor_tensor(
-                        out=dst[:, done], in0=dst[:, done], in1=gain1[:, t * S : (t + 1) * S][:, done], op=MULT
+                        out=h1[s][:, done], in0=h1[s][:, done], in1=gain1[:, t * S : (t + 1) * S][:, done], op=MULT
                     )
 
-        def respond2(s, b, pair):
-            g, t = divmod(s, 4)
-            dst = h2[t]
+        def filter2(s, b_halves, pair):
+            g, t = divmod(s, PACK)
             for half, bank in enumerate(pair):
                 cols = slice(BANK * half, BANK * (half + 1))
                 for a in range(2):
-                    c0 = 512 * a + 128 * t
+                    stationary = slice(PASS * a + P * t, PASS * a + P * (t + 1))
                     nc.tensor.matmul_mx(
                         out=bank[:],
-                        lhsT=w2_w[g][:, c0 : c0 + 128].bitcast(FP8X4),
-                        lhsT_scale=w2_s[g][:, c0 : c0 + 128],
+                        lhsT=w2_w[g][:, stationary].bitcast(FP8X4),
+                        lhsT_scale=w2_s[g][:, stationary],
                         rhs=v2_w[a][:, cols].bitcast(FP8X4),
                         rhs_scale=v2_s[4 * a : P, cols],
                         start=(a == 0), stop=(a == 1),
                     )
-                nc.scalar.copy(out=b[half], in_=bank[:])
-                nc.scalar.activation(out=dst[:, cols], in_=bank[:], func=ACT.Exp, scale=-0.2)
+                nc.scalar.copy(out=b_halves[half], in_=bank[:])
+                nc.scalar.activation(out=h2[t][:, cols], in_=bank[:], func=ACT.Exp, scale=-0.2)
 
         def halves(b):
             return [b[:, 0:BANK], b[:, BANK:S]]
 
         def calibrate2(s, b, cols=slice(0, S)):
-            t = s % 4
+            t = s % PACK
             nc.gpsimd.tensor_tensor(out=b, in0=b, in1=gain2[:, t * S : (t + 1) * S][:, cols], op=MULT)
 
         def decay2(s, b, cols=slice(0, S)):
-            dst = h2[s % 4][:, cols]
+            dst = h2[s % PACK][:, cols]
             nc.gpsimd.tensor_tensor(out=dst, in0=dst, in1=b, op=MULT)
 
-        def prepare2(s):
+        def make_h2(s):
             b = rows[s % 2][:, 0:S]
-            respond2(s, halves(b), next_banks())
+            filter2(s, halves(b), bank_pairs[(s + 1) % 2])
             calibrate2(s, b)
             decay2(s, b)
 
@@ -225,105 +224,109 @@ def tile_list_neutrino_tube_weave_kernel(
             n = S // pieces
             for i in range(pieces):
                 offsets = idx[2][:, i * n // 16 : (i + 1) * n // 16]
-                nc.vector.tensor_copy(pages[s % 5][:].indirect(offsets), h1[s][:, i * n : (i + 1) * n])
+                nc.vector.tensor_copy(pages[s % PAGES][:].indirect(offsets), h1[s][:, i * n : (i + 1) * n])
 
         def scatter2(s):
-            nc.vector.tensor_copy(pages[s % 5][:].indirect(idx[3][:]), h2[s % 4][:])
+            nc.vector.tensor_copy(pages[s % PAGES][:].indirect(idx[3][:]), h2[s % PACK][:])
 
         def accept(engine, s, c0, c1):
             cols = slice(BANK * c0, BANK * c1)
             engine.tensor_tensor(
-                out=planes[s // 4][:, c0:c1, s % 4, :],
-                in0=pages[s % 5][:, cols].rearrange("p (c m) -> p c m", m=BANK),
+                out=planes[s // PACK][:, c0:c1, s % PACK, :],
+                in0=pages[s % PAGES][:, cols].rearrange("p (c m) -> p c m", m=BANK),
                 in1=rows[s % 2][:, cols].rearrange("p (c m) -> p c m", m=BANK),
                 op=MULT,
             )
 
-        def accept_slow(s):
-            accept(nc.gpsimd, s, 0, 2)
-            accept(nc.gpsimd, s, 2, 4)
-            if s % 4 < 2:
+        def accept_on_gpsimd(s):
+            accept(nc.gpsimd, s, 0, CHUNKS // 2)
+            accept(nc.gpsimd, s, CHUNKS // 2, CHUNKS)
+            if s % PACK < 2:
                 load_acc(s + 2)
 
         def weave(copy, g, c):
-            dst = woven[g][:, 2048 * c : 2048 * (c + 1)]
+            dst = woven[g][:, PACK * BANK * c : PACK * BANK * (c + 1)]
             copy(
-                out=dst.rearrange("p (c i t) -> p c t i", i=4, t=4),
-                in_=planes[g][:, c, :, :].rearrange("p t (c i) -> p c t i", i=4),
+                out=dst.rearrange("p (u i t) -> p u t i", i=4, t=PACK),
+                in_=planes[g][:, c, :, :].rearrange("p t (u i) -> p u t i", i=4),
             )
 
         def quantise_z(g, c0, c1):
-            src = woven[g][:, 2048 * c0 : 2048 * c1]
+            src = woven[g][:, PACK * BANK * c0 : PACK * BANK * c1]
             cols = slice(T2 * g + BANK * c0, T2 * g + BANK * c1)
             nc.vector.quantize_mx(out=z_w[:, cols].bitcast(FP8X4), scales=z_s[:, cols], in_=src)
 
+        def out_bank(c, n):
+            return banks[(4 + 2 * c + n) % 8]
+
         def last_product(g, c):
             cols = slice(T2 * g + BANK * c, T2 * g + BANK * (c + 1))
-            for n in range(2):
+            for n in range(N // P):
                 nc.tensor.matmul_mx(
-                    out=banks[(4 + 2 * c + n) % 8][:],
-                    lhsT=w3_w[:, g, 128 * n : 128 * (n + 1)].bitcast(FP8X4),
-                    lhsT_scale=w3_s[4 * g : P, 128 * n : 128 * (n + 1)],
+                    out=out_bank(c, n)[:],
+                    lhsT=w3_w[:, g, P * n : P * (n + 1)].bitcast(FP8X4),
+                    lhsT_scale=w3_s[4 * g : P, P * n : P * (n + 1)],
                     rhs=z_w[:, cols].bitcast(FP8X4),
                     rhs_scale=z_s[:, cols],
                     start=(g == 0), stop=(g == 1),
                 )
 
         def store(c):
-            for n in range(2):
+            for n in range(N // P):
                 stage = h1[c][:, BANK * n : BANK * (n + 1)]
                 copy = nc.scalar.copy if n == 0 else nc.vector.tensor_copy
-                copy(out=stage, in_=banks[(4 + 2 * c + n) % 8][:])
+                copy(out=stage, in_=out_bank(c, n)[:])
                 queue = nc.scalar if n == 0 else nc.sync
-                queue.dma_start(out=out[128 * n : 128 * (n + 1), BANK * c : BANK * (c + 1)], in_=stage)
+                queue.dma_start(out=out[P * n : P * (n + 1), BANK * c : BANK * (c + 1)], in_=stage)
 
-        prepare1(0, pieces=2)
-        prepare1(1)
+        make_h1(0, pieces=2)
+        make_h1(1)
         scatter1(0, pieces=2)
-        prepare1(2)
-        prepare1(3)
+        make_h1(2)
+        make_h1(3)
         scatter1(1)
-        prepare1(4)
+        make_h1(4)
         scatter1(4)
-        gain2 = tile("gain2", [P, 4 * S], F32)
-        load_gain(gain2, wg2, 0, 4)
-        quantise_w2(0)
-        quantise_w2(1)
-        planes = [wide_tile("planes0", [P, 4, 4, BANK], BF16, 0)]
-        woven = [tile("woven0", [P, 4 * T2], BF16, tag="wide2")]
-        z_w = wide_tile("z_w", [P, 2 * T2], U32, WIDE)
-        for s in range(5, 8):
-            prepare1(s)
-        prepare2(0)
+        for s in range(5, SLICES):
+            make_h1(s)
+        gain2 = tile("gain2", [P, PACK * S], F32)
+        load_gain(gain2, wg2, 0, PACK)
+        w2_w[0] = tile("w2_w0", [P, 2 * PASS], U32, tag="h1_4")
+        quantise_w2(0, placed("w2_bf16_0", [P, 2 * PACK * PASS], BF16, across_pages))
+        for i in range(2):
+            pages[2 + i] = placed("page%d" % (2 + i), [P, T2], F32, 2 * REGION + i * REGION // 2)
+        planes = [placed("planes0", [P, CHUNKS, PACK, BANK], BF16, 0)]
+        woven = [tile("woven0", [P, PACK * T2], BF16)]
+        make_h2(0)
         scatter1(2)
-        prepare2(1)
+        make_h2(1)
+        quantise_w2(1, tile("w2_bf16_1", [P, 2 * PACK * PASS], BF16))
+        z_w = placed("z_w", [P, 2 * T2], U32, REGION)
         scatter1(3)
-        prepare2(2)
+        make_h2(2)
         load_acc(0)
         scatter2(0)
-        prepare2(3)
+        make_h2(3)
         load_acc(1)
-        accept_slow(0)
-        scatter2(1)
-        accept_slow(1)
-        scatter2(2)
-        accept_slow(2)
-        scatter2(3)
-        respond2(4, halves(rows[0]), banks[0:2])
-        accept_slow(3)
+        for s in range(3):
+            accept_on_gpsimd(s)
+            scatter2(s + 1)
+        filter2(4, halves(rows[0]), bank_pairs[0])
+        accept_on_gpsimd(3)
         calibrate2(4, rows[0][:, 0:S])
         decay2(4, rows[0][:, 0:S])
-        for c in range(4):
+        for c in range(CHUNKS):
             weave(nc.scalar.copy, 0, c)
+
         for s in (5, 6):
-            respond2(s, halves(spare[s % 2]), banks[0:2])
+            filter2(s, halves(spare_b[s % 2]), bank_pairs[0])
         for step in (calibrate2, decay2):
             for s in (5, 6):
-                step(s, spare[s % 2][:])
+                step(s, spare_b[s % 2][:])
         for s in (5, 6, 7):
             scatter1(s)
         last_b = [rows[half][:, 0:BANK] for half in range(2)]
-        respond2(7, last_b, banks[2:4])
+        filter2(7, last_b, bank_pairs[1])
         for step in (calibrate2, decay2):
             for half in range(2):
                 step(7, last_b[half], slice(BANK * half, BANK * (half + 1)))
@@ -333,21 +336,19 @@ def tile_list_neutrino_tube_weave_kernel(
         load_acc(5)
         scatter2(4)
         z_s = tile("z_s", [P, 2 * T2], U8, tag="h2_0")
-        quantise_z(0, 0, 2)
-        quantise_z(0, 2, 4)
-        planes.append(tile("planes1", [P, 4, 4, BANK], BF16, tag="wide2"))
-        woven.append(wide_tile("woven1", [P, 4 * T2], BF16, 0))
-        for c in range(4):
+        quantise_z(0, 0, CHUNKS // 2)
+        quantise_z(0, CHUNKS // 2, CHUNKS)
+        planes.append(tile("planes1", [P, CHUNKS, PACK, BANK], BF16, tag="woven0"))
+        woven.append(placed("woven1", [P, PACK * T2], BF16, 0))
+        for c in range(CHUNKS):
             last_product(0, c)
-        accept_slow(4)
-        scatter2(5)
-        accept_slow(5)
-        scatter2(6)
-        accept_slow(6)
-        scatter2(7)
-        for c in range(4):
-            accept(nc.vector, 7, c, c + 1)
-        for c in range(4):
+        for s in range(4, SLICES - 1):
+            accept_on_gpsimd(s)
+            scatter2(s + 1)
+
+        for c in range(CHUNKS):
+            accept(nc.vector, SLICES - 1, c, c + 1)
+        for c in range(CHUNKS):
             weave(nc.scalar.copy if c % 2 == 0 else nc.vector.tensor_copy, 1, c)
         for c in (0, 1, 3, 2):
             quantise_z(1, c, c + 1)

@@ -22,8 +22,8 @@ PASS = P * PACK
 BANK = 512
 CHUNKS = T2 // BANK
 SLICES = H // P
-PAGES = 5
-REGION = 4 * T
+KIB = 1024
+CHUNK = 256
 
 
 def tile_list_neutrino_tube_weave_kernel(
@@ -33,50 +33,51 @@ def tile_list_neutrino_tube_weave_kernel(
     nc = tc.nc
     with ExitStack() as ctx:
         lists = ctx.enter_context(tc.tile_pool(name="lists", bufs=1))
-        sb = ctx.enter_context(tc.tile_pool(name="sb", bufs=1))
         shared = ctx.enter_context(tc.tile_pool(name="shared", bufs=1))
         psum = ctx.enter_context(tc.psum_pool(name="psum", bufs=1))
 
-        def tile(name, shape, dtype, tag=None):
-            return sb.tile(shape, dtype, name=name, tag=tag or name, align_bytes=64)
-
-        def placed(name, shape, dtype, offset, align=64):
-            return shared.tile(shape, dtype, name=name, align_bytes=align, offset=offset)
+        def placed(name, shape, dtype, kib, shift=0, align=64):
+            return shared.tile(shape, dtype, name=name, align_bytes=align, offset=kib * KIB + shift)
 
         idx = [lists.tile([P, S // 16], U16, name="idx%d" % i) for i in range(4)]
         banks = [psum.tile([P, BANK], F32, name="bank%d" % b) for b in range(8)]
 
-        seed = placed("seed", [P, 2 * SLICES], F32, REGION - 32, align=32)
-        tab_w = [placed("tab_w%d" % a, [P, T], I32, REGION * a) for a in range(2)]
-        across_pages = 2 * REGION + REGION // 4
-        w1_raw = tile("w1_raw", [P, 2, H // 2], I32, tag="page1")
-        tab2_w = [tile("tab2_w%d" % a, [P, TC], I32, tag="page%d" % a) for a in range(2)]
-        tab_s = tile("tab_s", [P, T], U8, tag="gain1")
-        tab2_s = tile("tab2_s", [P, TC], U8, tag="gain2")
-        w1_s_raw = tile("w1_s_raw", [P, 2, H], U8)
-        w1_w = [tile("w1_w0", [P, 2, H], U8), placed("w1_w1", [P, 2, H], U8, across_pages)]
-        w1_s = [tile("w1_s0", [P, 2, PASS], U8), tile("w1_s1", [P, 2, PASS], U8, tag="w2_bf16_1")]
-        w3_s = tile("w3_s", [P, N], U8)
-        v_w = [tile("v_w%d" % a, [P, S], U32) for a in range(2)]
-        v2_w = [tile("v2_w%d" % a, [P, S], U32) for a in range(2)]
-        v_s = [tile("v_s%d" % a, [P, S], U8) for a in range(2)]
-        v2_s = tile("v2_s", [P, S], U8)
-        w2_w = [None, tile("w2_w1", [P, 2 * PASS], U32)]
-        w2_s = [tile("w2_s%d" % g, [P, 2 * PASS], U8) for g in range(2)]
-        rows = [tile("rows%d" % i, [P, T2], F32) for i in range(2)]
-        h1 = [tile("h1_%d" % s, [P, S], F32) for s in range(SLICES)]
-        h2 = [tile("h2_%d" % t, [P, S], F32) for t in range(PACK)]
-        spare_b = [tile("spare_b%d" % i, [P, S], F32) for i in range(2)]
-        one = tile("one", [P, 1], F32)
-        pages = [None] * (PAGES - 1) + [tile("page4", [P, T2], F32)]
+        at_v2b, at_a, at_g, at_b, at_c, at_d = 0, 4, 20, 24, 40, 56
+        at_page = [72, 88, 100, 108, 80, 120, 72, 0]
+        at_x, at_y = 96, 116
+        at_h1 = [136, 140, at_x, at_b + 8, 152, 156, 144, 160]
+        at_h2 = [at_a, at_a + 8, 128, 184, 152, 140, 176, 148]
+        at_bb = [at_a + 4, at_a + 12, 132, 180, 164, 168, at_b, at_h1[0]]
+        at_mid = [at_y, 172]
+        at_acc = [at_c, at_c + 8, 222, at_c, at_bb[2], None, 12, 20]
+        at_v, at_vs, at_v2, at_v2s = 188, 196, 198, 202
+        at_w1, at_w1s, at_w1sr, at_w2, at_w2s, at_w3s, at_w2b = 203, 222, 209, 211, 215, 217, 218
 
-        zero = tile("zero", [P, 2 * SLICES], F32)
+        seed = placed("seed", [P, 2 * SLICES], F32, at_g, shift=-96, align=32)
+        tab_w = [placed("tab_w%d" % a, [P, T], I32, (at_g, at_a)[a], shift=-64) for a in range(2)]
+        w1_raw = placed("w1_raw", [P, 2, H // 2], I32, at_page[4])
+        tab2_w = [placed("tab2_w%d" % a, [P, TC], I32, at_page[4 * a]) for a in range(2)]
+        tab_s = placed("tab_s", [P, T], U8, at_c)
+        tab2_s = placed("tab2_s", [P, TC], U8, at_d)
+        w1_s_raw = placed("w1_s_raw", [P, 2, H], U8, at_w1sr)
+        w1_w = [placed("w1_w%d" % g, [P, 2, H], U8, at_w1 + 2 * g) for g in range(2)]
+        w1_s = [placed("w1_s%d" % g, [P, 2, PASS], U8, at_w1s + g) for g in range(2)]
+        w3_s = placed("w3_s", [P, N], U8, at_w3s)
+        zero = placed("zero", [P, 2 * SLICES], F32, at_w3s, shift=512)
+        v_w = [placed("v_w%d" % a, [P, S], U32, at_v + 4 * a) for a in range(2)]
+        v2_w = [placed("v2_w0", [P, S], U32, at_v2)]
+        v_s = [placed("v_s%d" % a, [P, S], U8, at_vs + a) for a in range(2)]
+        v2_s = placed("v2_s", [P, S], U8, at_v2s)
+        w2_s = [placed("w2_s%d" % g, [P, 2 * PASS], U8, at_w2s + g) for g in range(2)]
+        w2_w = [placed("w2_w0", [P, 2 * PASS], U32, at_w2), None]
+        one = placed("one", [P, 1], F32, at_w3s, shift=768)[:]
+
         nc.vector.memset(tab_s[:].bitcast(I32), 0)
         nc.vector.memset(seed[:], 1.0)
         nc.scalar.activation(out=zero[:], in_=seed[:], func=ACT.Ln)
         for cleared in (w1_s_raw[:].rearrange("p a c -> p (a c)"), tab2_s[:], v_s[1][:], w3_s[:]):
             nc.vector.memset(cleared.bitcast(I32), 0)
-        nc.vector.memset(one[:], 1.0)
+        nc.vector.memset(one, 1.0)
 
         def load_packed_scales(queue, dst, scales):
             for quad in range(4):
@@ -88,31 +89,28 @@ def tile_list_neutrino_tube_weave_kernel(
         def words(src):
             return src.rearrange("p t i -> p (t i)").bitcast(I32)
 
-        def load_gain(dst, wg, t0, t1):
+        def load_gain(dst, wg, c0, c1):
             view = wg.rearrange("(m t) j -> m (t j)", t=PACK)
             for quad in (0, 2, 1, 3):
-                nc.sync.dma_start(
-                    out=dst[32 * quad : 32 * quad + 32, t0 * S : t1 * S], in_=view[:, t0 * S : t1 * S]
-                )
+                nc.sync.dma_start(out=dst[32 * quad : 32 * quad + 32, c0:c1], in_=view[:, c0:c1])
 
-        nc.sync.dma_start(idx[0][:], offs)
-        nc.sync.dma_start(out=w1_raw[:], in_=w1_words.bitcast(I32).rearrange("a p c -> p a c"))
-        load_packed_scales(nc.sync, tab_s, tab_scales)
-        for i, src in ((1, offs2), (2, offs3), (3, offs4)):
+        for i, src in enumerate((offs, offs2, offs3, offs4)):
             nc.sync.dma_start(idx[i][:], src)
+        nc.sync.dma_start(out=w1_raw[:], in_=w1_words.bitcast(I32).rearrange("a p c -> p a c"))
         nc.sync.dma_start(out=tab2_w[0][:], in_=words(tab2_words[0]))
+        load_packed_scales(nc.sync, tab_s, tab_scales)
         nc.sync.dma_start(out=tab_w[0][:], in_=words(tab_words[0]))
-        for quad in range(4):
+        for r in range(4):
             nc.sync.dma_start(
-                out=w1_s_raw[32 * quad : 32 * quad + 4, :, :].bitcast(I32),
-                in_=w1_scales[:, 4 * quad : 4 * quad + 4, :].bitcast(I32).rearrange("a r c -> r a c"),
+                out=w1_s_raw[r:P:32, :, :].bitcast(I32),
+                in_=w1_scales[:, r:16:4, :].bitcast(I32).rearrange("a q c -> q a c"),
             )
-        nc.sync.dma_start(out=tab_w[1][:], in_=words(tab_words[1]))
         load_packed_scales(nc.sync, tab2_s, tab2_scales)
+        nc.sync.dma_start(out=tab_w[1][:], in_=words(tab_words[1]))
         load_packed_scales(nc.gpsimd, w3_s, w3_scales)
 
         def load_w2(g):
-            dst = placed("w2_raw%d" % g, [P, 2 * PACK * PASS], F32, REGION * g)
+            dst = placed("w2_raw%d" % g, [P, 2 * PACK * PASS], F32, (at_b, at_a)[g])
             for a in range(2):
                 nc.sync.dma_start(
                     out=dst[:, PACK * PASS * a : PACK * PASS * (a + 1)].rearrange("p (j c) -> p j c", j=PACK),
@@ -120,51 +118,76 @@ def tile_list_neutrino_tube_weave_kernel(
                 )
             return dst
 
-        def load_acc(s):
+        rows = [[] for s in range(SLICES)]
+
+        def acc_rows(s):
             g, t = divmod(s, PACK)
-            src = acc[PASS * g : PASS * (g + 1), :].rearrange("(p t) m -> t p m", t=PACK)
-            nc.sync.dma_start(out=rows[s % 2][:], in_=src[t])
+            return acc[PASS * g : PASS * (g + 1), :].rearrange("(p t) m -> t p m", t=PACK)[t]
+
+        def load_acc(s):
+            whole = placed("acc%d" % s, [P, T2], F32, at_acc[s])
+            nc.sync.dma_start(out=whole[:], in_=acc_rows(s))
+            rows[s].append((0, whole))
+
+        def load_acc_half(s, half, kib):
+            part = placed("acc%d_%d" % (s, half), [P, S], F32, kib)
+            nc.sync.dma_start(out=part[:], in_=acc_rows(s)[:, S * half : S * (half + 1)])
+            rows[s].append((S * half, part))
 
         for g in range(2):
             nc.vector.tensor_copy(
                 out=w1_w[g][:].bitcast(U16).rearrange("p a (t m) -> p a t m", t=PACK),
                 in_=w1_raw[:, :, PASS // 2 * g : PASS // 2 * (g + 1)].bitcast(U16).rearrange("p a (m t) -> p a t m", t=PACK),
             )
-        nc.sync.dma_start(out=tab2_w[1][:], in_=words(tab2_words[1]))
         nc.vector.tensor_copy(v2_w[0][:], tab2_w[0][:].bitcast(U32).indirect(idx[1][:]))
         nc.vector.tensor_copy(v_s[0][:], tab_s[:].indirect(idx[0][:]))
         nc.gpsimd.dma_start(out=v_s[1][0:112, :].bitcast(I32), in_=v_s[0][4:116, :].bitcast(I32))
-        gain1 = tile("gain1", [P, PACK * S], F32)
-        for t0, t1 in ((0, 1), (1, 2), (2, 4)):
-            load_gain(gain1, wg1, t0, t1)
+        gain1 = placed("gain1", [P, PACK * S], F32, at_c)
+        nc.sync.dma_start(out=tab2_w[1][:], in_=words(tab2_words[1]))
+        load_gain(gain1, wg1, 0, BANK)
+        load_gain(gain1, wg1, BANK, S)
         nc.vector.tensor_copy(v_w[0][:], tab_w[0][:].bitcast(U32).indirect(idx[0][:]))
         for g in range(2):
             nc.vector.tensor_copy(
                 out=w1_s[g][:].rearrange("p a (t m) -> p a t m", t=PACK),
                 in_=w1_s_raw[:, :, PASS * g : PASS * (g + 1)].rearrange("p a (m t) -> p a t m", t=PACK),
             )
-        nc.vector.tensor_copy(v_w[1][:], tab_w[1][:].bitcast(U32).indirect(idx[0][:]))
         nc.vector.tensor_copy(v2_s[:], tab2_s[:].indirect(idx[1][:]))
-        nc.vector.tensor_copy(v2_w[1][:], tab2_w[1][:].bitcast(U32).indirect(idx[1][:]))
+        for half in range(2):
+            nc.vector.tensor_copy(
+                v_w[1][:, BANK * half : BANK * (half + 1)],
+                tab_w[1][:].bitcast(U32).indirect(idx[0][:, BANK // 16 * half : BANK // 16 * (half + 1)]),
+            )
 
-        w2_raw = [load_w2(g) for g in range(2)]
-        for a in range(2):
-            pages[a] = tile("page%d" % a, [P, T2], F32)
+        v2_w.append(placed("v2_w1", [P, S], U32, at_v2b))
+        nc.vector.tensor_copy(v2_w[1][:], tab2_w[1][:].bitcast(U32).indirect(idx[1][:]))
+        w2_raw = [load_w2(0), None]
+        for t in range(1, PACK):
+            load_gain(gain1, wg1, t * S, (t + 1) * S)
+        gain2 = placed("gain2", [P, PACK * S], F32, at_d)
+        load_gain(gain2, wg2, 0, S)
+        w2_raw[1] = load_w2(1)
+        load_gain(gain2, wg2, S, PACK * S)
+
+        def round_w2(g, a, rounded):
+            cols = slice(PACK * PASS * a, PACK * PASS * (a + 1))
+            nc.scalar.copy(
+                out=rounded[:, cols].rearrange("p (t m j) -> p m t j", t=PACK, j=PACK),
+                in_=w2_raw[g][:, cols].rearrange("p (j m t) -> p m t j", j=PACK, t=PACK),
+            )
 
         def quantise_w2(g, rounded):
-            for a in range(2):
-                cols = slice(PACK * PASS * a, PACK * PASS * (a + 1))
-                nc.scalar.copy(
-                    out=rounded[:, cols].rearrange("p (t m j) -> p m t j", t=PACK, j=PACK),
-                    in_=w2_raw[g][:, cols].rearrange("p (j m t) -> p m t j", j=PACK, t=PACK),
-                )
             nc.vector.quantize_mx(out=w2_w[g][:].bitcast(FP8X4), scales=w2_s[g][:], in_=rounded[:])
 
         bank_pairs = [banks[0:2], banks[2:4]]
+        h1 = [None] * SLICES
+        h2 = [None] * SLICES
+        bb = [None] * SLICES
+        pages = [None] * SLICES
 
-        def make_h1(s, pieces=1):
+        def filter1(s, raw, log, by_halves=False):
             g, t = divmod(s, PACK)
-            for half, bank in enumerate(bank_pairs[(s + 1) % 2]):
+            for half, bank in enumerate(bank_pairs[1 - g]):
                 cols = slice(BANK * half, BANK * (half + 1))
                 for a in range(2):
                     nc.tensor.matmul_mx(
@@ -176,19 +199,27 @@ def tile_list_neutrino_tube_weave_kernel(
                         start=(a == 0), stop=(a == 1),
                     )
                 column = 2 * s + half
-                nc.scalar.activation(
-                    out=h1[s][:, cols], in_=bank[:], func=ACT.Square, bias=zero[:, column : column + 1]
-                )
-                if pieces == 2 or half == 1:
-                    done = cols if pieces == 2 else slice(0, S)
-                    nc.scalar.activation(out=h1[s][:, done], in_=h1[s][:, done], func=ACT.Ln, bias=one[:])
-                    nc.gpsimd.tensor_tensor(
-                        out=h1[s][:, done], in0=h1[s][:, done], in1=gain1[:, t * S : (t + 1) * S][:, done], op=MULT
-                    )
+                square = raw[half] if by_halves else raw[:, cols]
+                nc.scalar.activation(out=square, in_=bank[:], func=ACT.Square, bias=zero[:, column : column + 1])
+                if by_halves:
+                    nc.scalar.activation(out=log[half], in_=square, func=ACT.Ln, bias=one)
+            if not by_halves:
+                nc.scalar.activation(out=log[:], in_=raw[:], func=ACT.Ln, bias=one)
 
-        def filter2(s, b_halves, pair):
+        def calibrate1(s, dst, raw, cols=slice(0, S)):
+            t = s % PACK
+            nc.gpsimd.tensor_tensor(out=dst, in0=raw, in1=gain1[:, t * S : (t + 1) * S][:, cols], op=MULT)
+
+        def make_h1(s):
+            h1[s] = placed("h1_%d" % s, [P, S], F32, at_h1[s])
+            filter1(s, h1[s], h1[s])
+            calibrate1(s, h1[s][:], h1[s][:])
+
+        def filter2(s):
             g, t = divmod(s, PACK)
-            for half, bank in enumerate(pair):
+            h2[s] = placed("h2_%d" % s, [P, S], F32, at_h2[s])
+            bb[s] = placed("b_%d" % s, [P, S], F32, at_bb[s])
+            for half, bank in enumerate(bank_pairs[(s + 1) % 2]):
                 cols = slice(BANK * half, BANK * (half + 1))
                 for a in range(2):
                     stationary = slice(PASS * a + P * t, PASS * a + P * (t + 1))
@@ -200,157 +231,209 @@ def tile_list_neutrino_tube_weave_kernel(
                         rhs_scale=v2_s[4 * a : P, cols],
                         start=(a == 0), stop=(a == 1),
                     )
-                nc.scalar.copy(out=b_halves[half], in_=bank[:])
-                nc.scalar.activation(out=h2[t][:, cols], in_=bank[:], func=ACT.Exp, scale=-0.2)
+                nc.scalar.activation(out=h2[s][:, cols], in_=bank[:], func=ACT.Exp, scale=-0.2)
+                nc.scalar.copy(out=bb[s][:, cols], in_=bank[:])
 
-        def halves(b):
-            return [b[:, 0:BANK], b[:, BANK:S]]
+        mid = [None] * SLICES
 
-        def calibrate2(s, b, cols=slice(0, S)):
+        def decay2(s):
+            mid[s] = placed("mid%d" % s, [P, S], F32, at_mid[s % 2])
+            nc.gpsimd.tensor_tensor(out=mid[s][:], in0=h2[s][:], in1=bb[s][:], op=MULT)
+
+        def calibrate2(s, kib=None):
             t = s % PACK
-            nc.gpsimd.tensor_tensor(out=b, in0=b, in1=gain2[:, t * S : (t + 1) * S][:, cols], op=MULT)
+            h2[s] = placed("h2_done%d" % s, [P, S], F32, at_h2[s] if kib is None else kib)
+            nc.gpsimd.tensor_tensor(out=h2[s][:], in0=mid[s][:], in1=gain2[:, t * S : (t + 1) * S], op=MULT)
 
-        def decay2(s, b, cols=slice(0, S)):
-            dst = h2[s % PACK][:, cols]
-            nc.gpsimd.tensor_tensor(out=dst, in0=dst, in1=b, op=MULT)
+        def new_page(s):
+            pages[s] = placed("page%d" % s, [P, T2], F32, at_page[s])
 
-        def make_h2(s):
-            b = rows[s % 2][:, 0:S]
-            filter2(s, halves(b), bank_pairs[(s + 1) % 2])
-            calibrate2(s, b)
-            decay2(s, b)
-
-        def scatter1(s, pieces=1):
-            n = S // pieces
-            for i in range(pieces):
-                offsets = idx[2][:, i * n // 16 : (i + 1) * n // 16]
-                nc.vector.tensor_copy(pages[s % PAGES][:].indirect(offsets), h1[s][:, i * n : (i + 1) * n])
+        def scatter1(s):
+            nc.vector.tensor_copy(pages[s][:].indirect(idx[2][:]), h1[s][:])
 
         def scatter2(s):
-            nc.vector.tensor_copy(pages[s % PAGES][:].indirect(idx[3][:]), h2[s % PACK][:])
+            nc.vector.tensor_copy(pages[s][:].indirect(idx[3][:]), h2[s][:])
 
-        def accept(engine, s, c0, c1):
-            cols = slice(BANK * c0, BANK * c1)
+        planes = [None, None]
+        woven = [None, None]
+
+        def accept(engine, s, m0, m1):
+            first, part = [(at, part) for at, part in rows[s] if at <= m0][-1]
             engine.tensor_tensor(
-                out=planes[s // PACK][:, c0:c1, s % PACK, :],
-                in0=pages[s % PAGES][:, cols].rearrange("p (c m) -> p c m", m=BANK),
-                in1=rows[s % 2][:, cols].rearrange("p (c m) -> p c m", m=BANK),
+                out=planes[s // PACK][:, s % PACK, m0:m1],
+                in0=pages[s][:, m0:m1],
+                in1=part[:, m0 - first : m1 - first],
                 op=MULT,
             )
 
-        def accept_on_gpsimd(s):
-            accept(nc.gpsimd, s, 0, CHUNKS // 2)
-            accept(nc.gpsimd, s, CHUNKS // 2, CHUNKS)
-            if s % PACK < 2:
-                load_acc(s + 2)
+        def accept_halves(s):
+            accept(nc.gpsimd, s, 0, S)
+            accept(nc.gpsimd, s, S, T2)
 
-        def weave(copy, g, c):
-            dst = woven[g][:, PACK * BANK * c : PACK * BANK * (c + 1)]
+        def weave(copy, g, m0, m1):
             copy(
-                out=dst.rearrange("p (u i t) -> p u t i", i=4, t=PACK),
-                in_=planes[g][:, c, :, :].rearrange("p t (u i) -> p u t i", i=4),
+                out=woven[g][:, PACK * m0 : PACK * m1].rearrange("p (u i t) -> p u t i", i=4, t=PACK),
+                in_=planes[g][:, :, m0:m1].rearrange("p t (u i) -> p u t i", i=4),
             )
 
-        def quantise_z(g, c0, c1):
-            src = woven[g][:, PACK * BANK * c0 : PACK * BANK * c1]
-            cols = slice(T2 * g + BANK * c0, T2 * g + BANK * c1)
-            nc.vector.quantize_mx(out=z_w[:, cols].bitcast(FP8X4), scales=z_s[:, cols], in_=src)
+        z_w = [None, None]
+        z_s = [None, None]
 
-        def out_bank(c, n):
-            return banks[(4 + 2 * c + n) % 8]
+        def quantise_z(g, m0, m1):
+            nc.vector.quantize_mx(
+                out=z_w[g][:, m0:m1].bitcast(FP8X4), scales=z_s[g][:, m0:m1], in_=woven[g][:, PACK * m0 : PACK * m1]
+            )
 
         def last_product(g, c):
-            cols = slice(T2 * g + BANK * c, T2 * g + BANK * (c + 1))
+            cols = slice(CHUNK * c, CHUNK * (c + 1))
             for n in range(N // P):
                 nc.tensor.matmul_mx(
-                    out=out_bank(c, n)[:],
+                    out=banks[c][:, CHUNK * n : CHUNK * (n + 1)],
                     lhsT=w3_w[:, g, P * n : P * (n + 1)].bitcast(FP8X4),
                     lhsT_scale=w3_s[4 * g : P, P * n : P * (n + 1)],
-                    rhs=z_w[:, cols].bitcast(FP8X4),
-                    rhs_scale=z_s[:, cols],
-                    start=(g == 0), stop=(g == 1),
+                    rhs=z_w[g][:, cols].bitcast(FP8X4),
+                    rhs_scale=z_s[g][:, cols],
+                    start=(g == 0 and n == 0), stop=(g == 1 and n == N // P - 1),
                 )
 
-        def store(c):
-            for n in range(N // P):
-                stage = h1[c][:, BANK * n : BANK * (n + 1)]
-                copy = nc.scalar.copy if n == 0 else nc.vector.tensor_copy
-                copy(out=stage, in_=out_bank(c, n)[:])
-                queue = nc.scalar if n == 0 else nc.sync
-                queue.dma_start(out=out[P * n : P * (n + 1), BANK * c : BANK * (c + 1)], in_=stage)
+        def store(c, copy):
+            stage = placed("stage%d" % c, [P, BANK], F32, at_d + 2 * c)
+            copy(out=stage[:], in_=banks[c][:])
+            nc.sync.dma_start(
+                out=out.rearrange("(n p) m -> p n m", p=P)[:, :, CHUNK * c : CHUNK * (c + 1)],
+                in_=stage[:].rearrange("p (n m) -> p n m", m=CHUNK),
+            )
 
-        make_h1(0, pieces=2)
-        make_h1(1)
-        scatter1(0, pieces=2)
-        make_h1(2)
-        make_h1(3)
-        scatter1(1)
+        halves = (slice(0, BANK), slice(BANK, S))
+        first = [placed("h1_0%d" % i, [P, BANK], F32, at_h1[0] + 2 * i)[:] for i in range(2)]
+        filter1(0, first, first, by_halves=True)
+        for half, cols in enumerate(halves):
+            calibrate1(0, first[half], first[half], cols)
         make_h1(4)
+        new_page(0)
+        for half in range(2):
+            offsets = idx[2][:, BANK // 16 * half : BANK // 16 * (half + 1)]
+            nc.vector.tensor_copy(pages[0][:].indirect(offsets), first[half])
+        make_h1(1)
+        new_page(4)
         scatter1(4)
-        for s in range(5, SLICES):
-            make_h1(s)
-        gain2 = tile("gain2", [P, PACK * S], F32)
-        load_gain(gain2, wg2, 0, PACK)
-        w2_w[0] = tile("w2_w0", [P, 2 * PASS], U32, tag="h1_4")
-        quantise_w2(0, placed("w2_bf16_0", [P, 2 * PACK * PASS], BF16, across_pages))
-        for i in range(2):
-            pages[2 + i] = placed("page%d" % (2 + i), [P, T2], F32, 2 * REGION + i * REGION // 2)
-        planes = [placed("planes0", [P, CHUNKS, PACK, BANK], BF16, 0)]
-        woven = [tile("woven0", [P, PACK * T2], BF16)]
-        make_h2(0)
-        scatter1(2)
-        make_h2(1)
-        quantise_w2(1, tile("w2_bf16_1", [P, 2 * PACK * PASS], BF16))
-        z_w = placed("z_w", [P, 2 * T2], U32, REGION)
-        scatter1(3)
-        make_h2(2)
-        load_acc(0)
-        scatter2(0)
-        make_h2(3)
-        load_acc(1)
-        for s in range(3):
-            accept_on_gpsimd(s)
-            scatter2(s + 1)
-        filter2(4, halves(rows[0]), bank_pairs[0])
-        accept_on_gpsimd(3)
-        calibrate2(4, rows[0][:, 0:S])
-        decay2(4, rows[0][:, 0:S])
-        for c in range(CHUNKS):
-            weave(nc.scalar.copy, 0, c)
-
-        for s in (5, 6):
-            filter2(s, halves(spare_b[s % 2]), bank_pairs[0])
-        for step in (calibrate2, decay2):
-            for s in (5, 6):
-                step(s, spare_b[s % 2][:])
-        for s in (5, 6, 7):
-            scatter1(s)
-        last_b = [rows[half][:, 0:BANK] for half in range(2)]
-        filter2(7, last_b, bank_pairs[1])
-        for step in (calibrate2, decay2):
-            for half in range(2):
-                step(7, last_b[half], slice(BANK * half, BANK * (half + 1)))
-        load_acc(4)
-        w3_w = tile("w3_w", [P, 2, N], I32, tag="w2_w1")
+        make_h1(5)
+        rounded = placed("w2_bf16_0", [P, 2 * PACK * PASS], BF16, at_x - 2)
+        round_w2(0, 0, rounded)
+        round_w2(0, 1, rounded)
+        quantise_w2(0, rounded)
+        for s in (2, 6):
+            raw = placed("raw%d" % s, [P, S], F32, at_b + 2 * s)
+            h1[s] = placed("h1_%d" % s, [P, S], F32, at_h1[s])
+            filter1(s, raw, raw)
+            calibrate1(s, h1[s][:], raw[:])
+        make_h1(3)
+        raw7 = placed("raw7", [P, S], F32, at_y)
+        h1[7] = placed("h1_7", [P, S], F32, at_h1[7])
+        filter1(7, raw7, h1[7])
+        calibrate1(7, h1[7][:], h1[7][:])
+        w3_w = placed("w3_w", [P, 2, N], I32, at_w1)
         nc.sync.dma_start(out=w3_w[:], in_=w3_words.rearrange("a p c i -> p a (c i)").bitcast(I32))
-        load_acc(5)
-        scatter2(4)
-        z_s = tile("z_s", [P, 2 * T2], U8, tag="h2_0")
-        quantise_z(0, 0, CHUNKS // 2)
-        quantise_z(0, CHUNKS // 2, CHUNKS)
-        planes.append(tile("planes1", [P, CHUNKS, PACK, BANK], BF16, tag="woven0"))
-        woven.append(placed("woven1", [P, PACK * T2], BF16, 0))
-        for c in range(CHUNKS):
+        for s in (1, 2):
+            new_page(s)
+            scatter1(s)
+        rounded = placed("w2_bf16_1", [P, 2 * PACK * PASS], BF16, at_y - 2)
+        round_w2(1, 0, rounded)
+        round_w2(1, 1, rounded)
+        w2_w[1] = placed("w2_w1", [P, 2 * PASS], U32, at_w2b)
+        quantise_w2(1, rounded)
+        for s in (3, 5):
+            new_page(s)
+            scatter1(s)
+        load_acc(0)
+        load_acc(1)
+        load_acc(2)
+        filter2(0)
+        decay2(0)
+        for s in range(1, 6):
+            filter2(s)
+            decay2(s)
+            calibrate2(s - 1)
+            scatter2(s - 1)
+        filter2(6)
+        decay2(6)
+        filter2(7)
+        planes[0] = placed("planes0", [P, PACK, T2], BF16, at_b)
+        accept(nc.gpsimd, 0, 0, T2)
+        load_acc(3)
+        new_page(6)
+        scatter1(6)
+        accept(nc.gpsimd, 1, 0, T2)
+        calibrate2(5)
+        decay2(7)
+        load_acc(4)
+        accept(nc.gpsimd, 2, 0, T2)
+        accept_halves(3)
+        load_acc_half(5, 0, at_c)
+        calibrate2(6)
+        woven[0] = placed("woven0", [P, PACK * T2], BF16, at_a + 2)
+        for m in range(0, T2, BANK):
+            weave(nc.scalar.copy, 0, m, m + BANK)
+        for s in (5, 6):
+            scatter2(s)
+        planes[1] = placed("planes1", [P, PACK, T2], BF16, at_page[2])
+        accept(nc.gpsimd, 4, 0, T2)
+        accept(nc.gpsimd, 5, 0, S)
+        z_w[0] = placed("z_w0", [P, T2], U32, at_v)
+        z_s[0] = placed("z_s0", [P, T2], U8, at_h2[6])
+        quantise_z(0, 0, S)
+        quantise_z(0, S, T2)
+        load_acc_half(5, 1, at_acc[7])
+        load_acc(6)
+        for c in range(T2 // CHUNK):
             last_product(0, c)
-        for s in range(4, SLICES - 1):
-            accept_on_gpsimd(s)
-            scatter2(s + 1)
+        new_page(7)
+        scatter1(7)
+        calibrate2(7, at_a + 4)
+        scatter2(7)
+        accept(nc.gpsimd, 5, S, T2)
+        load_acc(7)
+        accept(nc.gpsimd, 6, 0, T2)
+        woven[1] = placed("woven1", [P, PACK * T2], BF16, at_page[0])
+        z_w[1] = placed("z_w1", [P, T2], U32, at_v)
+        z_s[1] = placed("z_s1", [P, T2], U8, at_vs)
 
-        for c in range(CHUNKS):
-            accept(nc.vector, SLICES - 1, c, c + 1)
-        for c in range(CHUNKS):
-            weave(nc.scalar.copy if c % 2 == 0 else nc.vector.tensor_copy, 1, c)
-        for c in (0, 1, 3, 2):
-            quantise_z(1, c, c + 1)
+        def accept_last(c0, c1):
+            accept(nc.vector, SLICES - 1, CHUNK * c0, CHUNK * c1)
+
+        def weave_last(copy, c):
+            weave(copy, 1, CHUNK * c, CHUNK * (c + 1))
+
+        def finish(c):
+            quantise_z(1, CHUNK * c, CHUNK * (c + 1))
             last_product(1, c)
-            store(c)
+
+        on_s, on_v = nc.scalar.copy, nc.vector.tensor_copy
+        accept_last(0, 1)
+        accept_last(1, 2)
+        weave_last(on_s, 0)
+        accept_last(2, 4)
+        weave_last(on_v, 1)
+        weave_last(on_s, 2)
+        accept_last(4, 6)
+        finish(0)
+        finish(1)
+        weave_last(on_v, 3)
+        store(0, on_s)
+        store(1, on_s)
+        finish(2)
+        accept_last(6, 8)
+        finish(3)
+        weave_last(on_s, 5)
+        weave_last(on_v, 4)
+        store(2, on_s)
+        store(3, on_s)
+        weave_last(on_v, 6)
+        finish(4)
+        finish(5)
+        weave_last(on_v, 7)
+        finish(6)
+        finish(7)
+        for c in (4, 5, 6):
+            store(c, on_s)
+        store(7, on_v)

@@ -42,7 +42,7 @@ def tile_list_neutrino_tube_weave_kernel(
         idx = [lists.tile([P, S // 16], U16, name="idx%d" % i) for i in range(4)]
         banks = [psum.tile([P, BANK], F32, name="bank%d" % b) for b in range(8)]
 
-        at_v2b, at_a, at_g, at_b, at_c, at_d = 0, 4, 20, 24, 40, 56
+        at_v2b, at_a, at_g, at_b, at_c, at_d = 0, 4, 20, 24, 56, 40
         at_page = [72, 88, 100, 108, 80, 120, 72, 0]
         at_x, at_y = 96, 116
         at_h1 = [136, 140, at_x, at_b + 8, 152, 156, 144, 160]
@@ -53,12 +53,13 @@ def tile_list_neutrino_tube_weave_kernel(
         at_v, at_vs, at_v2, at_v2s = 188, 196, 198, 202
         at_w1, at_w1s, at_w1sr, at_w2, at_w2s, at_w3s, at_w2b = 203, 222, 209, 211, 215, 217, 218
 
-        seed = placed("seed", [P, 2 * SLICES], F32, at_g, shift=-96, align=32)
+        seed = placed("seed", [P, T + 2 * SLICES], F32, at_g, shift=-96, align=32)[:, 0 : 2 * SLICES]
         tab_w = [placed("tab_w%d" % a, [P, T], I32, (at_g, at_a)[a], shift=-64) for a in range(2)]
         w1_raw = placed("w1_raw", [P, 2, H // 2], I32, at_page[4])
-        tab2_w = [placed("tab2_w%d" % a, [P, TC], I32, at_page[4 * a]) for a in range(2)]
+        tab2_w = [placed("tab2_w0", [P, TC], I32, at_g + 16, shift=-64), placed("tab2_w1", [P, TC], I32, at_page[4])]
         tab_s = placed("tab_s", [P, T], U8, at_c)
-        tab2_s = placed("tab2_s", [P, TC], U8, at_d)
+        picked = [placed("picked%d" % i, [P, S], U8, 230 + i) for i in range(2)]
+        tab2_s = placed("tab2_s", [P, TC], U8, at_d + 8)
         w1_s_raw = placed("w1_s_raw", [P, 2, H], U8, at_w1sr)
         w1_w = [placed("w1_w%d" % g, [P, 2, H], U8, at_w1 + 2 * g) for g in range(2)]
         w1_s = [placed("w1_s%d" % g, [P, 2, PASS], U8, at_w1s + g) for g in range(2)]
@@ -73,9 +74,10 @@ def tile_list_neutrino_tube_weave_kernel(
         one = placed("one", [P, 1], F32, at_w3s, shift=768)[:]
 
         nc.vector.memset(tab_s[:].bitcast(I32), 0)
-        nc.vector.memset(seed[:], 1.0)
-        nc.scalar.activation(out=zero[:], in_=seed[:], func=ACT.Ln)
-        for cleared in (w1_s_raw[:].rearrange("p a c -> p (a c)"), tab2_s[:], v_s[1][:], w3_s[:]):
+        nc.vector.memset(tab2_s[:].bitcast(I32), 0)
+        nc.vector.memset(seed, 1.0)
+        nc.scalar.activation(out=zero[:], in_=seed, func=ACT.Ln)
+        for cleared in (w1_s_raw[:].rearrange("p a c -> p (a c)"), v_s[0][:], v_s[1][:], v2_s[:], w3_s[:]):
             nc.vector.memset(cleared.bitcast(I32), 0)
         nc.vector.memset(one, 1.0)
 
@@ -84,6 +86,16 @@ def tile_list_neutrino_tube_weave_kernel(
                 queue.dma_start(
                     out=dst[32 * quad : 32 * quad + 8, :].bitcast(I32),
                     in_=scales[:, 4 * quad : 4 * quad + 4, :].bitcast(I32),
+                )
+
+        def load_spread(dst, scales):
+            nc.sync.dma_start(out=dst[0:P:4, :].bitcast(I32), in_=scales.bitcast(I32).rearrange("a q t -> (a q) t"))
+
+        def deal(queue, dst, first, src, a):
+            for r in range(4):
+                queue.dma_start(
+                    out=dst[first + r : P : 32, :].bitcast(I32),
+                    in_=src[64 * a + 4 * r : 64 * (a + 1) : 16, :].bitcast(I32),
                 )
 
         def words(src):
@@ -97,15 +109,15 @@ def tile_list_neutrino_tube_weave_kernel(
         for i, src in enumerate((offs, offs2, offs3, offs4)):
             nc.sync.dma_start(idx[i][:], src)
         nc.sync.dma_start(out=w1_raw[:], in_=w1_words.bitcast(I32).rearrange("a p c -> p a c"))
+        load_spread(tab_s, tab_scales)
+        load_spread(tab2_s, tab2_scales)
         nc.sync.dma_start(out=tab2_w[0][:], in_=words(tab2_words[0]))
-        load_packed_scales(nc.sync, tab_s, tab_scales)
         nc.sync.dma_start(out=tab_w[0][:], in_=words(tab_words[0]))
         for r in range(4):
             nc.sync.dma_start(
                 out=w1_s_raw[r:P:32, :, :].bitcast(I32),
                 in_=w1_scales[:, r:16:4, :].bitcast(I32).rearrange("a q c -> q a c"),
             )
-        load_packed_scales(nc.sync, tab2_s, tab2_scales)
         nc.sync.dma_start(out=tab_w[1][:], in_=words(tab_words[1]))
         load_packed_scales(nc.gpsimd, w3_s, w3_scales)
 
@@ -139,9 +151,11 @@ def tile_list_neutrino_tube_weave_kernel(
                 out=w1_w[g][:].bitcast(U16).rearrange("p a (t m) -> p a t m", t=PACK),
                 in_=w1_raw[:, :, PASS // 2 * g : PASS // 2 * (g + 1)].bitcast(U16).rearrange("p a (m t) -> p a t m", t=PACK),
             )
+        nc.vector.tensor_copy(picked[0][:], tab_s[:].indirect(idx[0][:]))
+        for a in range(2):
+            deal((nc.scalar, nc.gpsimd)[a], v_s[a], 0, picked[0], a)
+        nc.vector.tensor_copy(picked[1][:], tab2_s[:].indirect(idx[1][:]))
         nc.vector.tensor_copy(v2_w[0][:], tab2_w[0][:].bitcast(U32).indirect(idx[1][:]))
-        nc.vector.tensor_copy(v_s[0][:], tab_s[:].indirect(idx[0][:]))
-        nc.gpsimd.dma_start(out=v_s[1][0:112, :].bitcast(I32), in_=v_s[0][4:116, :].bitcast(I32))
         gain1 = placed("gain1", [P, PACK * S], F32, at_c)
         nc.sync.dma_start(out=tab2_w[1][:], in_=words(tab2_words[1]))
         load_gain(gain1, wg1, 0, BANK)
@@ -152,7 +166,6 @@ def tile_list_neutrino_tube_weave_kernel(
                 out=w1_s[g][:].rearrange("p a (t m) -> p a t m", t=PACK),
                 in_=w1_s_raw[:, :, PASS * g : PASS * (g + 1)].rearrange("p a (m t) -> p a t m", t=PACK),
             )
-        nc.vector.tensor_copy(v2_s[:], tab2_s[:].indirect(idx[1][:]))
         for half in range(2):
             nc.vector.tensor_copy(
                 v_w[1][:, BANK * half : BANK * (half + 1)],
@@ -167,6 +180,8 @@ def tile_list_neutrino_tube_weave_kernel(
         gain2 = placed("gain2", [P, PACK * S], F32, at_d)
         load_gain(gain2, wg2, 0, S)
         w2_raw[1] = load_w2(1)
+        for a in range(2):
+            deal(nc.sync, v2_s, 4 * a, picked[1], a)
         load_gain(gain2, wg2, S, PACK * S)
 
         def round_w2(g, a, rounded):
@@ -199,7 +214,7 @@ def tile_list_neutrino_tube_weave_kernel(
                         start=(a == 0), stop=(a == 1),
                     )
                 column = 2 * s + half
-                square = raw[half] if by_halves else raw[:, cols]
+                square = placed("square%d" % half, [P, BANK], F32, raw)[:] if by_halves else raw[:, cols]
                 nc.scalar.activation(out=square, in_=bank[:], func=ACT.Square, bias=zero[:, column : column + 1])
                 if by_halves:
                     nc.scalar.activation(out=log[half], in_=square, func=ACT.Ln, bias=one)
@@ -306,7 +321,7 @@ def tile_list_neutrino_tube_weave_kernel(
 
         halves = (slice(0, BANK), slice(BANK, S))
         first = [placed("h1_0%d" % i, [P, BANK], F32, at_h1[0] + 2 * i)[:] for i in range(2)]
-        filter1(0, first, first, by_halves=True)
+        filter1(0, at_mid[1], first, by_halves=True)
         for half, cols in enumerate(halves):
             calibrate1(0, first[half], first[half], cols)
         make_h1(4)
@@ -317,7 +332,9 @@ def tile_list_neutrino_tube_weave_kernel(
         make_h1(1)
         new_page(4)
         scatter1(4)
-        make_h1(5)
+        h1[5] = placed("h1_5", [P, S], F32, at_h1[5])
+        filter1(5, placed("raw5", [P, S], F32, at_x), h1[5])
+        calibrate1(5, h1[5][:], h1[5][:])
         rounded = placed("w2_bf16_0", [P, 2 * PACK * PASS], BF16, at_x - 2)
         round_w2(0, 0, rounded)
         round_w2(0, 1, rounded)

@@ -45,27 +45,26 @@ def tile_list_neutrino_tube_weave_kernel(
         at_v2b, at_a, at_g, at_b, at_c, at_d = 0, 4, 20, 24, 56, 40
         at_page = [72, 88, 100, 108, 80, 120, 72, 0]
         at_x, at_y = 96, 116
-        at_h1 = [136, 140, at_x, at_b + 8, 152, 156, 144, 160]
-        at_h2 = [at_a, at_a + 8, 128, 184, 152, 140, 176, 148]
+        at_h1 = [136, 140, at_x, at_b + 8, 144, 156, 152, 160]
+        at_h2 = [at_a, at_a + 8, 128, 184, 144, 140, 176, 148]
         at_bb = [at_a + 4, at_a + 12, 132, 180, 164, 168, at_b, at_h1[0]]
         at_mid = [at_y, 172]
         at_acc = [at_c, at_c + 8, 222, at_c, at_bb[2], None, 12, 20]
         at_v, at_vs, at_v2, at_v2s = 188, 196, 198, 202
-        at_w1, at_w1s, at_w1sr, at_w2, at_w2s, at_w3s, at_w2b = 203, 222, 209, 211, 215, 217, 218
+        at_w1, at_w1s, at_w1sr, at_w2, at_w2s, at_w3s, at_w2b = 203, 207, 209, 211, 215, 217, 218
 
         seed = placed("seed", [P, T + 2 * SLICES], F32, at_g, shift=-96, align=32)[:, 0 : 2 * SLICES]
         tab_w = [placed("tab_w%d" % a, [P, T], I32, (at_g, at_a)[a], shift=-64) for a in range(2)]
-        w1_raw = placed("w1_raw", [P, 2, H // 2], I32, at_page[4])
-        tab2_w = [placed("tab2_w0", [P, TC], I32, at_g + 16, shift=-64), placed("tab2_w1", [P, TC], I32, at_page[4])]
+        w1_raw = placed("w1_raw", [P, 2, H // 2], I32, at_page[4] - 4)
+        tab2_w = [placed("tab2_w0", [P, TC], I32, at_g + 16, shift=-64), placed("tab2_w1", [P, TC], I32, at_page[4] - 4)]
         tab_s = placed("tab_s", [P, T], U8, at_c)
         picked = [placed("picked%d" % i, [P, S], U8, 230 + i) for i in range(2)]
         tab2_s = placed("tab2_s", [P, TC], U8, at_d + 8)
-        w1_s_raw = placed("w1_s_raw", [P, 2, H], U8, at_w1sr)
+        w1_s_raw = placed("w1_s_raw", [P, 2, H], U8, at_v + 4)
         w1_w = [placed("w1_w%d" % g, [P, 2, H], U8, at_w1 + 2 * g) for g in range(2)]
-        w1_s = [placed("w1_s%d" % g, [P, 2, PASS], U8, at_w1s + g) for g in range(2)]
-        w3_s = placed("w3_s", [P, N], U8, at_w3s)
+        w1_s = [placed("w1_s%d" % g, [P, 2, PASS], U8, (at_w1s, at_acc[2])[g]) for g in range(2)]
         zero = placed("zero", [P, 2 * SLICES], F32, at_w3s, shift=512)
-        v_w = [placed("v_w%d" % a, [P, S], U32, at_v + 4 * a) for a in range(2)]
+        v_w = [placed("v_w0", [P, S], U32, at_v), None]
         v2_w = [placed("v2_w0", [P, S], U32, at_v2)]
         v_s = [placed("v_s%d" % a, [P, S], U8, at_vs + a) for a in range(2)]
         v2_s = placed("v2_s", [P, S], U8, at_v2s)
@@ -77,7 +76,7 @@ def tile_list_neutrino_tube_weave_kernel(
         nc.vector.memset(tab2_s[:].bitcast(I32), 0)
         nc.vector.memset(seed, 1.0)
         nc.scalar.activation(out=zero[:], in_=seed, func=ACT.Ln)
-        for cleared in (w1_s_raw[:].rearrange("p a c -> p (a c)"), v_s[0][:], v_s[1][:], v2_s[:], w3_s[:]):
+        for cleared in (w1_s_raw[:].rearrange("p a c -> p (a c)"), v_s[0][:], v_s[1][:], v2_s[:]):
             nc.vector.memset(cleared.bitcast(I32), 0)
         nc.vector.memset(one, 1.0)
 
@@ -91,9 +90,9 @@ def tile_list_neutrino_tube_weave_kernel(
         def load_spread(dst, scales):
             nc.sync.dma_start(out=dst[0:P:4, :].bitcast(I32), in_=scales.bitcast(I32).rearrange("a q t -> (a q) t"))
 
-        def deal(queue, dst, first, src, a):
+        def deal(queues, dst, first, src, a):
             for r in range(4):
-                queue.dma_start(
+                queues[r].dma_start(
                     out=dst[first + r : P : 32, :].bitcast(I32),
                     in_=src[64 * a + 4 * r : 64 * (a + 1) : 16, :].bitcast(I32),
                 )
@@ -119,7 +118,6 @@ def tile_list_neutrino_tube_weave_kernel(
                 in_=w1_scales[:, r:16:4, :].bitcast(I32).rearrange("a q c -> q a c"),
             )
         nc.sync.dma_start(out=tab_w[1][:], in_=words(tab_words[1]))
-        load_packed_scales(nc.gpsimd, w3_s, w3_scales)
 
         def load_w2(g):
             dst = placed("w2_raw%d" % g, [P, 2 * PACK * PASS], F32, (at_b, at_a)[g])
@@ -153,19 +151,20 @@ def tile_list_neutrino_tube_weave_kernel(
             )
         nc.vector.tensor_copy(picked[0][:], tab_s[:].indirect(idx[0][:]))
         for a in range(2):
-            deal((nc.scalar, nc.gpsimd)[a], v_s[a], 0, picked[0], a)
+            deal([nc.scalar if 4 * a + r < 2 else nc.gpsimd for r in range(4)], v_s[a], 0, picked[0], a)
         nc.vector.tensor_copy(picked[1][:], tab2_s[:].indirect(idx[1][:]))
         nc.vector.tensor_copy(v2_w[0][:], tab2_w[0][:].bitcast(U32).indirect(idx[1][:]))
-        gain1 = placed("gain1", [P, PACK * S], F32, at_c)
-        nc.sync.dma_start(out=tab2_w[1][:], in_=words(tab2_words[1]))
-        load_gain(gain1, wg1, 0, BANK)
-        load_gain(gain1, wg1, BANK, S)
-        nc.vector.tensor_copy(v_w[0][:], tab_w[0][:].bitcast(U32).indirect(idx[0][:]))
         for g in range(2):
             nc.vector.tensor_copy(
                 out=w1_s[g][:].rearrange("p a (t m) -> p a t m", t=PACK),
                 in_=w1_s_raw[:, :, PASS * g : PASS * (g + 1)].rearrange("p a (m t) -> p a t m", t=PACK),
             )
+        gain1 = placed("gain1", [P, PACK * S], F32, at_c)
+        nc.sync.dma_start(out=tab2_w[1][:], in_=words(tab2_words[1]))
+        load_gain(gain1, wg1, 0, BANK)
+        load_gain(gain1, wg1, BANK, S)
+        nc.vector.tensor_copy(v_w[0][:], tab_w[0][:].bitcast(U32).indirect(idx[0][:]))
+        v_w[1] = placed("v_w1", [P, S], U32, at_v + 4)
         for half in range(2):
             nc.vector.tensor_copy(
                 v_w[1][:, BANK * half : BANK * (half + 1)],
@@ -181,7 +180,7 @@ def tile_list_neutrino_tube_weave_kernel(
         load_gain(gain2, wg2, 0, S)
         w2_raw[1] = load_w2(1)
         for a in range(2):
-            deal(nc.sync, v2_s, 4 * a, picked[1], a)
+            deal([nc.sync] * 4, v2_s, 4 * a, picked[1], a)
         load_gain(gain2, wg2, S, PACK * S)
 
         def round_w2(g, a, rounded):
@@ -321,7 +320,7 @@ def tile_list_neutrino_tube_weave_kernel(
 
         halves = (slice(0, BANK), slice(BANK, S))
         first = [placed("h1_0%d" % i, [P, BANK], F32, at_h1[0] + 2 * i)[:] for i in range(2)]
-        filter1(0, at_mid[1], first, by_halves=True)
+        filter1(0, at_h1[4] - 1, first, by_halves=True)
         for half, cols in enumerate(halves):
             calibrate1(0, first[half], first[half], cols)
         make_h1(4)
@@ -349,6 +348,8 @@ def tile_list_neutrino_tube_weave_kernel(
         h1[7] = placed("h1_7", [P, S], F32, at_h1[7])
         filter1(7, raw7, h1[7])
         calibrate1(7, h1[7][:], h1[7][:])
+        w3_s = w1_s[0][:, 0, 0:N]
+        load_packed_scales(nc.sync, w3_s, w3_scales)
         w3_w = placed("w3_w", [P, 2, N], I32, at_w1)
         nc.sync.dma_start(out=w3_w[:], in_=w3_words.rearrange("a p c i -> p a (c i)").bitcast(I32))
         for s in (1, 2):

@@ -24,6 +24,8 @@ CHUNKS = T2 // BANK
 SLICES = H // P
 KIB = 1024
 CHUNK = 256
+ON_SCALAR = 5
+LAG = 4
 
 
 def tile_list_neutrino_tube_weave_kernel(
@@ -42,14 +44,14 @@ def tile_list_neutrino_tube_weave_kernel(
         idx = [lists.tile([P, S // 16], U16, name="idx%d" % i) for i in range(4)]
         banks = [psum.tile([P, BANK], F32, name="bank%d" % b) for b in range(8)]
 
-        at_v2b, at_a, at_g, at_b, at_c, at_d = 0, 4, 20, 24, 56, 40
-        at_page = [72, 88, 100, 108, 80, 120, 72, 0]
-        at_x, at_y = 96, 116
-        at_h1 = [136, 140, at_x, at_b + 8, 144, 156, 152, 160]
+        at_v2b, at_a, at_g, at_b, at_c, at_d = 0, 4, 20, 28, 60, 44
+        at_page = [76, 92, 104, at_g, 84, 120, 76, at_b]
+        at_x, at_y = 100, 116
+        at_h1 = [136, 140, at_b + 4, at_b + 8, 144, 156, 152, 160]
         at_h2 = [at_a, at_a + 8, 128, 184, 144, 140, 176, 148]
         at_bb = [at_a + 4, at_a + 12, 132, 180, 164, 168, at_b, at_h1[0]]
         at_mid = [at_y, 172]
-        at_acc = [at_c, at_c + 8, 222, at_c, at_bb[2], None, 12, 20]
+        at_acc = [at_c, at_c + 8, 222, at_c + 8, at_bb[2], at_c + 8, 12, 222]
         at_v, at_vs, at_v2, at_v2s = 188, 196, 198, 202
         at_w1, at_w1s, at_w1sr, at_w2, at_w2s, at_w3s, at_w2b = 203, 207, 209, 211, 215, 217, 218
 
@@ -60,7 +62,7 @@ def tile_list_neutrino_tube_weave_kernel(
         tab_s = placed("tab_s", [P, T], U8, at_c)
         picked = [placed("picked%d" % i, [P, S], U8, 230 + i) for i in range(2)]
         tab2_s = placed("tab2_s", [P, TC], U8, at_d + 8)
-        w1_s_raw = placed("w1_s_raw", [P, 2, H], U8, at_v + 4)
+        w1_s_raw = placed("w1_s_raw", [P, 2, H], U8, at_x)
         w1_w = [placed("w1_w%d" % g, [P, 2, H], U8, at_w1 + 2 * g) for g in range(2)]
         w1_s = [placed("w1_s%d" % g, [P, 2, PASS], U8, (at_w1s, at_acc[2])[g]) for g in range(2)]
         zero = placed("zero", [P, 2 * SLICES], F32, at_w3s, shift=512)
@@ -120,7 +122,7 @@ def tile_list_neutrino_tube_weave_kernel(
         nc.sync.dma_start(out=tab_w[1][:], in_=words(tab_words[1]))
 
         def load_w2(g):
-            dst = placed("w2_raw%d" % g, [P, 2 * PACK * PASS], F32, (at_b, at_a)[g])
+            dst = placed("w2_raw%d" % g, [P, 2 * PACK * PASS], F32, (at_x - 2, at_a)[g], shift=64 * g)
             for a in range(2):
                 nc.sync.dma_start(
                     out=dst[:, PACK * PASS * a : PACK * PASS * (a + 1)].rearrange("p (j c) -> p j c", j=PACK),
@@ -193,32 +195,36 @@ def tile_list_neutrino_tube_weave_kernel(
         def quantise_w2(g, rounded):
             nc.vector.quantize_mx(out=w2_w[g][:].bitcast(FP8X4), scales=w2_s[g][:], in_=rounded[:])
 
+        halves = (slice(0, BANK), slice(BANK, S))
         bank_pairs = [banks[0:2], banks[2:4]]
         h1 = [None] * SLICES
         h2 = [None] * SLICES
         bb = [None] * SLICES
         pages = [None] * SLICES
 
-        def filter1(s, raw, log, by_halves=False):
+        def square1(s, half, dst):
             g, t = divmod(s, PACK)
-            for half, bank in enumerate(bank_pairs[1 - g]):
-                cols = slice(BANK * half, BANK * (half + 1))
-                for a in range(2):
-                    nc.tensor.matmul_mx(
-                        out=bank[:],
-                        lhsT=w1_w[g][:, a, 2 * P * t : 2 * P * (t + 1)].bitcast(FP4X4),
-                        lhsT_scale=w1_s[g][:, a, P * t : P * (t + 1)],
-                        rhs=v_w[a][:, cols].bitcast(FP8X4),
-                        rhs_scale=v_s[a][:, cols],
-                        start=(a == 0), stop=(a == 1),
-                    )
-                column = 2 * s + half
-                square = placed("square%d" % half, [P, BANK], F32, raw)[:] if by_halves else raw[:, cols]
-                nc.scalar.activation(out=square, in_=bank[:], func=ACT.Square, bias=zero[:, column : column + 1])
-                if by_halves:
-                    nc.scalar.activation(out=log[half], in_=square, func=ACT.Ln, bias=one)
-            if not by_halves:
-                nc.scalar.activation(out=log[:], in_=raw[:], func=ACT.Ln, bias=one)
+            bank = bank_pairs[1 - g][half]
+            cols = halves[half]
+            for a in range(2):
+                nc.tensor.matmul_mx(
+                    out=bank[:],
+                    lhsT=w1_w[g][:, a, 2 * P * t : 2 * P * (t + 1)].bitcast(FP4X4),
+                    lhsT_scale=w1_s[g][:, a, P * t : P * (t + 1)],
+                    rhs=v_w[a][:, cols].bitcast(FP8X4),
+                    rhs_scale=v_s[a][:, cols],
+                    start=(a == 0), stop=(a == 1),
+                )
+            column = 2 * s + half
+            nc.scalar.activation(out=dst, in_=bank[:], func=ACT.Square, bias=zero[:, column : column + 1])
+
+        def log1p(dst, src):
+            nc.scalar.activation(out=dst, in_=src, func=ACT.Ln, bias=one)
+
+        def filter1(s, raw, log):
+            for half, cols in enumerate(halves):
+                square1(s, half, raw[:, cols])
+            log1p(log[:], raw[:])
 
         def calibrate1(s, dst, raw, cols=slice(0, S)):
             t = s % PACK
@@ -271,10 +277,10 @@ def tile_list_neutrino_tube_weave_kernel(
         planes = [None, None]
         woven = [None, None]
 
-        def accept(engine, s, m0, m1):
+        def accept(engine, s, m0, m1, dst=None):
             first, part = [(at, part) for at, part in rows[s] if at <= m0][-1]
             engine.tensor_tensor(
-                out=planes[s // PACK][:, s % PACK, m0:m1],
+                out=planes[s // PACK][:, s % PACK, m0:m1] if dst is None else dst,
                 in0=pages[s][:, m0:m1],
                 in1=part[:, m0 - first : m1 - first],
                 op=MULT,
@@ -288,6 +294,24 @@ def tile_list_neutrino_tube_weave_kernel(
             copy(
                 out=woven[g][:, PACK * m0 : PACK * m1].rearrange("p (u i t) -> p u t i", i=4, t=PACK),
                 in_=planes[g][:, :, m0:m1].rearrange("p t (u i) -> p u t i", i=4),
+            )
+
+        def pair_up(m0, m1):
+            nc.scalar.copy(
+                out=pairs[:, 0, m0:m1, :].rearrange("p (u i) t -> p u t i", i=8),
+                in_=planes[1][:, 0:2, m0:m1].rearrange("p t (u i) -> p u t i", i=8),
+            )
+
+        def half_pair(m0, m1):
+            nc.scalar.copy(
+                out=pairs[:, 1, m0:m1, :],
+                in_=planes[1][:, 2, m0:m1].unsqueeze(2).to_broadcast([P, m1 - m0, 2]),
+            )
+
+        def weave_pairs(copy, word, m0, m1):
+            copy(
+                out=woven[1][:, PACK * m0 : PACK * m1].bitcast(word).rearrange("p (u i h) -> p u h i", i=4, h=2),
+                in_=pairs[:].rearrange("p h m t -> p h (m t)").bitcast(word)[:, :, m0:m1].rearrange("p h (u i) -> p u h i", i=4),
             )
 
         z_w = [None, None]
@@ -310,36 +334,34 @@ def tile_list_neutrino_tube_weave_kernel(
                     start=(g == 0 and n == 0), stop=(g == 1 and n == N // P - 1),
                 )
 
-        def store(c, copy):
+        def store(c, copy, queue):
             stage = placed("stage%d" % c, [P, BANK], F32, at_d + 2 * c)
             copy(out=stage[:], in_=banks[c][:])
-            nc.sync.dma_start(
+            queue.dma_start(
                 out=out.rearrange("(n p) m -> p n m", p=P)[:, :, CHUNK * c : CHUNK * (c + 1)],
                 in_=stage[:].rearrange("p (n m) -> p n m", m=CHUNK),
             )
 
-        halves = (slice(0, BANK), slice(BANK, S))
-        first = [placed("h1_0%d" % i, [P, BANK], F32, at_h1[0] + 2 * i)[:] for i in range(2)]
-        filter1(0, at_h1[4] - 1, first, by_halves=True)
-        for half, cols in enumerate(halves):
-            calibrate1(0, first[half], first[half], cols)
-        make_h1(4)
         new_page(0)
-        for half in range(2):
-            offsets = idx[2][:, BANK // 16 * half : BANK // 16 * (half + 1)]
-            nc.vector.tensor_copy(pages[0][:].indirect(offsets), first[half])
-        make_h1(1)
         new_page(4)
-        scatter1(4)
+        for (s, half), at_square in zip(((0, 0), (4, 0), (0, 1), (4, 1)), (1, 0, 2, 0)):
+            square = placed("square%d%d" % (s, half), [P, BANK], F32, at_h1[1] + at_square)[:]
+            part = placed("h1_%d%d" % (s, half), [P, BANK], F32, at_h1[s] + 2 * half)[:]
+            square1(s, half, square)
+            log1p(part, square)
+            calibrate1(s, part, part, halves[half])
+            offsets = idx[2][:, BANK // 16 * half : BANK // 16 * (half + 1)]
+            nc.vector.tensor_copy(pages[s][:].indirect(offsets), part)
+        make_h1(1)
         h1[5] = placed("h1_5", [P, S], F32, at_h1[5])
-        filter1(5, placed("raw5", [P, S], F32, at_x), h1[5])
+        filter1(5, placed("raw5", [P, S], F32, at_b), h1[5])
         calibrate1(5, h1[5][:], h1[5][:])
-        rounded = placed("w2_bf16_0", [P, 2 * PACK * PASS], BF16, at_x - 2)
+        rounded = placed("w2_bf16_0", [P, 2 * PACK * PASS], BF16, at_b)
         round_w2(0, 0, rounded)
         round_w2(0, 1, rounded)
         quantise_w2(0, rounded)
         for s in (2, 6):
-            raw = placed("raw%d" % s, [P, S], F32, at_b + 2 * s)
+            raw = placed("raw%d" % s, [P, S], F32, at_x + 3 * (s - 2))
             h1[s] = placed("h1_%d" % s, [P, S], F32, at_h1[s])
             filter1(s, raw, raw)
             calibrate1(s, h1[s][:], raw[:])
@@ -378,80 +400,69 @@ def tile_list_neutrino_tube_weave_kernel(
         filter2(7)
         planes[0] = placed("planes0", [P, PACK, T2], BF16, at_b)
         accept(nc.gpsimd, 0, 0, T2)
-        load_acc(3)
         new_page(6)
         scatter1(6)
         accept(nc.gpsimd, 1, 0, T2)
-        calibrate2(5)
+        load_acc(3)
+        calibrate2(5, at_acc[0])
         decay2(7)
         load_acc(4)
         accept(nc.gpsimd, 2, 0, T2)
+        load_acc(7)
         accept_halves(3)
-        load_acc_half(5, 0, at_c)
+        load_acc(5)
         calibrate2(6)
-        woven[0] = placed("woven0", [P, PACK * T2], BF16, at_a + 2)
+        woven[0] = placed("woven0", [P, PACK * T2], BF16, at_a)
         for m in range(0, T2, BANK):
             weave(nc.scalar.copy, 0, m, m + BANK)
         for s in (5, 6):
             scatter2(s)
-        planes[1] = placed("planes1", [P, PACK, T2], BF16, at_page[2])
+        planes[1] = placed("planes1", [P, PACK - 1, T2], BF16, at_h1[1])
+        pairs = placed("pairs", [P, 2, T2, 2], BF16, at_x)
         accept(nc.gpsimd, 4, 0, T2)
-        accept(nc.gpsimd, 5, 0, S)
+        accept(nc.gpsimd, 5, 0, T2)
+        pair_up(0, S)
+        pair_up(S, T2)
         z_w[0] = placed("z_w0", [P, T2], U32, at_v)
-        z_s[0] = placed("z_s0", [P, T2], U8, at_h2[6])
+        z_s[0] = placed("z_s0", [P, T2], U8, at_mid[0])
         quantise_z(0, 0, S)
         quantise_z(0, S, T2)
-        load_acc_half(5, 1, at_acc[7])
-        load_acc(6)
+        load_acc_half(6, 0, at_acc[6])
+        load_acc_half(6, 1, at_acc[6] + 4)
         for c in range(T2 // CHUNK):
             last_product(0, c)
         new_page(7)
         scatter1(7)
         calibrate2(7, at_a + 4)
         scatter2(7)
-        accept(nc.gpsimd, 5, S, T2)
-        load_acc(7)
-        accept(nc.gpsimd, 6, 0, T2)
+        accept_halves(6)
+        half_pair(0, T2)
         woven[1] = placed("woven1", [P, PACK * T2], BF16, at_page[0])
         z_w[1] = placed("z_w1", [P, T2], U32, at_v)
         z_s[1] = placed("z_s1", [P, T2], U8, at_vs)
 
         def accept_last(c0, c1):
-            accept(nc.vector, SLICES - 1, CHUNK * c0, CHUNK * c1)
+            accept(nc.vector, SLICES - 1, CHUNK * c0, CHUNK * c1, dst=pairs[:, 1, CHUNK * c0 : CHUNK * c1, 1])
 
-        def weave_last(copy, c):
-            weave(copy, 1, CHUNK * c, CHUNK * (c + 1))
+        def weave_last(on_scalar, c):
+            copy, word = (nc.scalar.copy, U32) if on_scalar else (nc.vector.tensor_copy, I32)
+            weave_pairs(copy, word, CHUNK * c, CHUNK * (c + 1))
 
         def finish(c):
             quantise_z(1, CHUNK * c, CHUNK * (c + 1))
             last_product(1, c)
 
-        on_s, on_v = nc.scalar.copy, nc.vector.tensor_copy
-        accept_last(0, 1)
-        accept_last(1, 2)
-        weave_last(on_s, 0)
-        accept_last(2, 4)
-        weave_last(on_v, 1)
-        weave_last(on_s, 2)
-        accept_last(4, 6)
-        finish(0)
-        finish(1)
-        weave_last(on_v, 3)
-        store(0, on_s)
-        store(1, on_s)
-        finish(2)
-        accept_last(6, 8)
-        finish(3)
-        weave_last(on_s, 5)
-        weave_last(on_v, 4)
-        store(2, on_s)
-        store(3, on_s)
-        weave_last(on_v, 6)
-        finish(4)
-        finish(5)
-        weave_last(on_v, 7)
-        finish(6)
-        finish(7)
-        for c in (4, 5, 6):
-            store(c, on_s)
-        store(7, on_v)
+        last = T2 // CHUNK
+        for c in range(last):
+            accept_last(c, c + 1)
+            if c < ON_SCALAR:
+                weave_last(True, c)
+            if c >= LAG:
+                finish(c - LAG)
+        for c in range(last - LAG, last):
+            if ON_SCALAR <= c + 1 < last:
+                weave_last(False, c + 1)
+            finish(c)
+        for c in range(last - 1):
+            store(c, nc.scalar.copy, nc.sync)
+        store(last - 1, nc.scalar.copy, nc.sync)

@@ -51,7 +51,7 @@ def tile_list_neutrino_tube_weave_kernel(
         at_h2 = [at_a, at_a + 8, 128, 184, 144, 140, 176, 148]
         at_bb = [at_a + 4, at_a + 12, 132, 180, 164, 168, at_b, at_h1[0]]
         at_mid = [at_y, 172]
-        at_acc = [at_c, at_c + 8, 222, at_c + 8, at_bb[2], at_c + 8, 12, 222]
+        at_acc = [at_c, at_c + 8, 222, at_c + 8, at_bb[2], at_c + 8, at_page[1], 222]
         at_v, at_vs, at_v2, at_v2s = 188, 196, 198, 202
         at_w1, at_w1s, at_w1sr, at_w2, at_w2s, at_w3s, at_w2b = 203, 207, 209, 211, 215, 217, 218
 
@@ -305,7 +305,7 @@ def tile_list_neutrino_tube_weave_kernel(
         def half_pair(m0, m1):
             nc.scalar.copy(
                 out=pairs[:, 1, m0:m1, :],
-                in_=planes[1][:, 2, m0:m1].unsqueeze(2).to_broadcast([P, m1 - m0, 2]),
+                in_=plane6[:, m0:m1].unsqueeze(2).to_broadcast([P, m1 - m0, 2]),
             )
 
         def weave_pairs(copy, word, m0, m1):
@@ -404,6 +404,7 @@ def tile_list_neutrino_tube_weave_kernel(
         scatter1(6)
         accept(nc.gpsimd, 1, 0, T2)
         load_acc(3)
+        load_acc(6)
         calibrate2(5, at_acc[0])
         decay2(7)
         load_acc(4)
@@ -417,7 +418,7 @@ def tile_list_neutrino_tube_weave_kernel(
             weave(nc.scalar.copy, 0, m, m + BANK)
         for s in (5, 6):
             scatter2(s)
-        planes[1] = placed("planes1", [P, PACK - 1, T2], BF16, at_h1[1])
+        planes[1] = placed("planes1", [P, 2, T2], BF16, at_h1[1])
         pairs = placed("pairs", [P, 2, T2, 2], BF16, at_x)
         accept(nc.gpsimd, 4, 0, T2)
         accept(nc.gpsimd, 5, 0, T2)
@@ -427,15 +428,14 @@ def tile_list_neutrino_tube_weave_kernel(
         z_s[0] = placed("z_s0", [P, T2], U8, at_mid[0])
         quantise_z(0, 0, S)
         quantise_z(0, S, T2)
-        load_acc_half(6, 0, at_acc[6])
-        load_acc_half(6, 1, at_acc[6] + 4)
         for c in range(T2 // CHUNK):
             last_product(0, c)
         new_page(7)
         scatter1(7)
         calibrate2(7, at_a + 4)
         scatter2(7)
-        accept_halves(6)
+        plane6 = placed("plane6", [P, T2], BF16, at_a + 8)
+        accept(nc.gpsimd, 6, 0, T2, dst=plane6[:])
         half_pair(0, T2)
         woven[1] = placed("woven1", [P, PACK * T2], BF16, at_page[0])
         z_w[1] = placed("z_w1", [P, T2], U32, at_v)

@@ -53,16 +53,17 @@ def tile_list_neutrino_tube_weave_kernel(
         at_mid = [at_y, 172]
         at_acc = [at_c, at_c + 8, 222, at_c + 8, at_bb[2], at_c + 8, at_page[1], 222]
         at_v, at_vs, at_v2, at_v2s = 188, 196, 198, 202
+        at_v2, at_v2b = at_v2b, at_v2
         at_w1, at_w1s, at_w1sr, at_w2, at_w2s, at_w3s, at_w2b = 203, 207, 209, 211, 215, 217, 218
 
-        seed = placed("seed", [P, T + 2 * SLICES], F32, at_g, shift=-96, align=32)[:, 0 : 2 * SLICES]
+        seed = placed("seed", [P, 2 * SLICES], F32, at_w3s, shift=640)[:]
         tab_w = [placed("tab_w%d" % a, [P, T], I32, (at_g, at_a)[a], shift=-64) for a in range(2)]
-        w1_raw = placed("w1_raw", [P, 2, H // 2], I32, at_page[4] - 4)
+        w1_raw = placed("w1_raw", [P, 2, H // 2], I32, at_a + 4)[:]
         tab2_w = [placed("tab2_w0", [P, TC], I32, at_g + 16, shift=-64), placed("tab2_w1", [P, TC], I32, at_page[4] - 4)]
-        tab_s = placed("tab_s", [P, T], U8, at_c)
+        tab_s = placed("tab_s", [P, T], U8, at_a)
         picked = [placed("picked%d" % i, [P, S], U8, 230 + i) for i in range(2)]
-        tab2_s = placed("tab2_s", [P, TC], U8, at_d + 8)
-        w1_s_raw = placed("w1_s_raw", [P, 2, H], U8, at_x)
+        tab2_s = placed("tab2_s", [P, TC], U8, at_bb[2])
+        w1_s_raw = placed("w1_s_raw", [P, 56 * KIB], U8, at_d - 1)[:, 0 : 2 * H].rearrange("p (a c) -> p a c", a=2)
         w1_w = [placed("w1_w%d" % g, [P, 2, H], U8, at_w1 + 2 * g) for g in range(2)]
         w1_s = [placed("w1_s%d" % g, [P, 2, PASS], U8, (at_w1s, at_acc[2])[g]) for g in range(2)]
         zero = placed("zero", [P, 2 * SLICES], F32, at_w3s, shift=512)
@@ -74,12 +75,15 @@ def tile_list_neutrino_tube_weave_kernel(
         w2_w = [placed("w2_w0", [P, 2 * PASS], U32, at_w2), None]
         one = placed("one", [P, 1], F32, at_w3s, shift=768)[:]
 
-        nc.vector.memset(tab_s[:].bitcast(I32), 0)
-        nc.vector.memset(tab2_s[:].bitcast(I32), 0)
+        nc.vector.memset(w1_s_raw.rearrange("p a c -> p (a c)").bitcast(I32), 0)
         nc.vector.memset(seed, 1.0)
         nc.scalar.activation(out=zero[:], in_=seed, func=ACT.Ln)
-        for cleared in (w1_s_raw[:].rearrange("p a c -> p (a c)"), v_s[0][:], v_s[1][:], v2_s[:]):
-            nc.vector.memset(cleared.bitcast(I32), 0)
+        nc.vector.memset(tab_s[64:P, :].bitcast(I32), 0)
+        nc.gpsimd.memset(tab_s[32:64, :].bitcast(I32), 0)
+        nc.vector.memset(tab2_s[0:64, :].bitcast(I32), 0)
+        nc.gpsimd.memset(tab2_s[96:P, :].bitcast(I32), 0)
+        for cleared in (v_s[0][:], v_s[1][:], v2_s[:]):
+            nc.gpsimd.memset(cleared.bitcast(I32), 0)
         nc.vector.memset(one, 1.0)
 
         def load_packed_scales(queue, dst, scales):
@@ -89,14 +93,14 @@ def tile_list_neutrino_tube_weave_kernel(
                     in_=scales[:, 4 * quad : 4 * quad + 4, :].bitcast(I32),
                 )
 
-        def load_spread(dst, scales):
-            nc.sync.dma_start(out=dst[0:P:4, :].bitcast(I32), in_=scales.bitcast(I32).rearrange("a q t -> (a q) t"))
+        def load_rows(dst, scales):
+            nc.sync.dma_start(out=dst.bitcast(I32), in_=scales.bitcast(I32).rearrange("a q t -> (a q) t"))
 
         def deal(queues, dst, first, src, a):
             for r in range(4):
                 queues[r].dma_start(
                     out=dst[first + r : P : 32, :].bitcast(I32),
-                    in_=src[64 * a + 4 * r : 64 * (a + 1) : 16, :].bitcast(I32),
+                    in_=src[16 * a + r : 16 * (a + 1) : 4, :].bitcast(I32),
                 )
 
         def words(src):
@@ -107,19 +111,17 @@ def tile_list_neutrino_tube_weave_kernel(
             for quad in (0, 2, 1, 3):
                 nc.sync.dma_start(out=dst[32 * quad : 32 * quad + 32, c0:c1], in_=view[:, c0:c1])
 
-        for i, src in enumerate((offs, offs2, offs3, offs4)):
-            nc.sync.dma_start(idx[i][:], src)
-        nc.sync.dma_start(out=w1_raw[:], in_=w1_words.bitcast(I32).rearrange("a p c -> p a c"))
-        load_spread(tab_s, tab_scales)
-        load_spread(tab2_s, tab2_scales)
-        nc.sync.dma_start(out=tab2_w[0][:], in_=words(tab2_words[0]))
-        nc.sync.dma_start(out=tab_w[0][:], in_=words(tab_words[0]))
+        nc.sync.dma_start(idx[0][:], offs)
+        load_rows(tab_s[0:32, :], tab_scales)
+        nc.sync.dma_start(out=w1_raw, in_=w1_words.bitcast(I32).rearrange("a p c -> p a c"))
         for r in range(4):
             nc.sync.dma_start(
                 out=w1_s_raw[r:P:32, :, :].bitcast(I32),
                 in_=w1_scales[:, r:16:4, :].bitcast(I32).rearrange("a q c -> q a c"),
             )
-        nc.sync.dma_start(out=tab_w[1][:], in_=words(tab_words[1]))
+        nc.sync.dma_start(out=tab_w[0][:], in_=words(tab_words[0]))
+        nc.sync.dma_start(idx[1][:], offs2)
+        load_rows(tab2_s[64:96, :], tab2_scales)
 
         def load_w2(g):
             dst = placed("w2_raw%d" % g, [P, 2 * PACK * PASS], F32, (at_x - 2, at_a)[g], shift=64 * g)
@@ -146,26 +148,29 @@ def tile_list_neutrino_tube_weave_kernel(
             nc.sync.dma_start(out=part[:], in_=acc_rows(s)[:, S * half : S * (half + 1)])
             rows[s].append((S * half, part))
 
+        nc.vector.tensor_copy(picked[0][:], tab_s[:].indirect(idx[0][:]))
+        for a in range(2):
+            deal([nc.scalar if 4 * a + r < 3 else nc.gpsimd for r in range(4)], v_s[a], 0, picked[0], a)
         for g in range(2):
             nc.vector.tensor_copy(
                 out=w1_w[g][:].bitcast(U16).rearrange("p a (t m) -> p a t m", t=PACK),
                 in_=w1_raw[:, :, PASS // 2 * g : PASS // 2 * (g + 1)].bitcast(U16).rearrange("p a (m t) -> p a t m", t=PACK),
             )
-        nc.vector.tensor_copy(picked[0][:], tab_s[:].indirect(idx[0][:]))
-        for a in range(2):
-            deal([nc.scalar if 4 * a + r < 2 else nc.gpsimd for r in range(4)], v_s[a], 0, picked[0], a)
-        nc.vector.tensor_copy(picked[1][:], tab2_s[:].indirect(idx[1][:]))
-        nc.vector.tensor_copy(v2_w[0][:], tab2_w[0][:].bitcast(U32).indirect(idx[1][:]))
         for g in range(2):
             nc.vector.tensor_copy(
                 out=w1_s[g][:].rearrange("p a (t m) -> p a t m", t=PACK),
                 in_=w1_s_raw[:, :, PASS * g : PASS * (g + 1)].rearrange("p a (m t) -> p a t m", t=PACK),
             )
+        nc.sync.dma_start(out=tab_w[1][:], in_=words(tab_words[1]))
         gain1 = placed("gain1", [P, PACK * S], F32, at_c)
+        nc.sync.dma_start(out=tab2_w[0][:], in_=words(tab2_words[0]))
         nc.sync.dma_start(out=tab2_w[1][:], in_=words(tab2_words[1]))
         load_gain(gain1, wg1, 0, BANK)
+        nc.sync.dma_start(idx[2][:], offs3)
         load_gain(gain1, wg1, BANK, S)
+        nc.sync.dma_start(idx[3][:], offs4)
         nc.vector.tensor_copy(v_w[0][:], tab_w[0][:].bitcast(U32).indirect(idx[0][:]))
+        nc.vector.tensor_copy(picked[1][:], tab2_s[:].indirect(idx[1][:]))
         v_w[1] = placed("v_w1", [P, S], U32, at_v + 4)
         for half in range(2):
             nc.vector.tensor_copy(
@@ -173,6 +178,7 @@ def tile_list_neutrino_tube_weave_kernel(
                 tab_w[1][:].bitcast(U32).indirect(idx[0][:, BANK // 16 * half : BANK // 16 * (half + 1)]),
             )
 
+        nc.vector.tensor_copy(v2_w[0][:], tab2_w[0][:].bitcast(U32).indirect(idx[1][:]))
         v2_w.append(placed("v2_w1", [P, S], U32, at_v2b))
         nc.vector.tensor_copy(v2_w[1][:], tab2_w[1][:].bitcast(U32).indirect(idx[1][:]))
         w2_raw = [load_w2(0), None]
@@ -182,7 +188,7 @@ def tile_list_neutrino_tube_weave_kernel(
         load_gain(gain2, wg2, 0, S)
         w2_raw[1] = load_w2(1)
         for a in range(2):
-            deal([nc.sync] * 4, v2_s, 4 * a, picked[1], a)
+            deal([nc.sync] * 4, v2_s, 4 * a, picked[1][64:96, :], a)
         load_gain(gain2, wg2, S, PACK * S)
 
         def round_w2(g, a, rounded):

@@ -51,15 +51,15 @@ def tile_list_neutrino_tube_weave_kernel(
         at_h2 = [at_a, at_a + 8, 128, 184, 144, 140, 176, 148]
         at_bb = [at_a + 4, at_a + 12, 132, 180, 164, 168, at_b, at_h1[0]]
         at_mid = [at_y, 172]
-        at_acc = [at_c, at_c + 8, 222, at_c + 8, at_bb[2], at_c + 8, at_page[1], 222]
+        at_acc = [at_c, at_c + 8, 222, at_c + 8, at_bb[2], at_c + 8, 222, at_page[1]]
         at_v, at_vs, at_v2, at_v2s = 188, 196, 198, 202
         at_v2, at_v2b = at_v2b, at_v2
         at_w1, at_w1s, at_w1sr, at_w2, at_w2s, at_w3s, at_w2b = 203, 207, 209, 211, 215, 217, 218
 
         seed = placed("seed", [P, 2 * SLICES], F32, at_w3s, shift=640)[:]
-        tab_w = [placed("tab_w%d" % a, [P, T], I32, (at_g, at_a)[a], shift=-64) for a in range(2)]
+        tab_w = [placed("tab_w%d" % a, [P, T], I32, (at_g, at_a)[a]) for a in range(2)]
         w1_raw = placed("w1_raw", [P, 2, H // 2], I32, at_a + 4)[:]
-        tab2_w = [placed("tab2_w0", [P, TC], I32, at_g + 16, shift=-64), placed("tab2_w1", [P, TC], I32, at_page[4] - 4)]
+        tab2_w = [placed("tab2_w0", [P, TC], I32, at_g + 16), placed("tab2_w1", [P, TC], I32, at_d)]
         tab_s = placed("tab_s", [P, T], U8, at_a)
         picked = [placed("picked%d" % i, [P, S], U8, 230 + i) for i in range(2)]
         tab2_s = placed("tab2_s", [P, TC], U8, at_bb[2])
@@ -138,9 +138,9 @@ def tile_list_neutrino_tube_weave_kernel(
             g, t = divmod(s, PACK)
             return acc[PASS * g : PASS * (g + 1), :].rearrange("(p t) m -> t p m", t=PACK)[t]
 
-        def load_acc(s):
-            whole = placed("acc%d" % s, [P, T2], F32, at_acc[s])
-            nc.sync.dma_start(out=whole[:], in_=acc_rows(s))
+        def load_acc(s, spare=0):
+            whole = placed("acc%d" % s, [P, T2 + spare], F32, at_acc[s])
+            nc.sync.dma_start(out=whole[:, 0:T2], in_=acc_rows(s))
             rows[s].append((0, whole))
 
         def load_acc_half(s, half, kib):
@@ -410,12 +410,12 @@ def tile_list_neutrino_tube_weave_kernel(
         scatter1(6)
         accept(nc.gpsimd, 1, 0, T2)
         load_acc(3)
-        load_acc(6)
+        load_acc(7)
         calibrate2(5, at_acc[0])
         decay2(7)
         load_acc(4)
         accept(nc.gpsimd, 2, 0, T2)
-        load_acc(7)
+        load_acc(6, S - CHUNK)
         accept_halves(3)
         load_acc(5)
         calibrate2(6)
@@ -430,18 +430,25 @@ def tile_list_neutrino_tube_weave_kernel(
         accept(nc.gpsimd, 5, 0, T2)
         pair_up(0, S)
         pair_up(S, T2)
-        z_w[0] = placed("z_w0", [P, T2], U32, at_v)
-        z_s[0] = placed("z_s0", [P, T2], U8, at_mid[0])
+        new_page(7)
+        scatter1(7)
+        plane6 = placed("plane6", [P, T2], BF16, at_acc[5])
+        h2[7] = rows[6][0][1][:, T2 - CHUNK : T2 - CHUNK + S]
+        late, early = slice(0, CHUNK), slice(CHUNK, S)
+
+        def calibrate_last(cols):
+            nc.gpsimd.tensor_tensor(out=h2[7][:, cols], in0=mid[7][:, cols], in1=gain2[:, 3 * S : 4 * S][:, cols], op=MULT)
+
+        calibrate_last(early)
+        accept(nc.gpsimd, 6, 0, T2, dst=plane6[:])
+        calibrate_last(late)
+        z_w[0] = placed("z_w0", [P, T2], U32, at_b + 8)
+        z_s[0] = placed("z_s0", [P, T2], U8, at_mid[1])
         quantise_z(0, 0, S)
         quantise_z(0, S, T2)
         for c in range(T2 // CHUNK):
             last_product(0, c)
-        new_page(7)
-        scatter1(7)
-        calibrate2(7, at_a + 4)
         scatter2(7)
-        plane6 = placed("plane6", [P, T2], BF16, at_a + 8)
-        accept(nc.gpsimd, 6, 0, T2, dst=plane6[:])
         half_pair(0, T2)
         woven[1] = placed("woven1", [P, PACK * T2], BF16, at_page[0])
         z_w[1] = placed("z_w1", [P, T2], U32, at_v)

@@ -194,8 +194,8 @@ def tile_list_neutrino_tube_weave_kernel(
         def round_w2(g, a, rounded):
             cols = slice(PACK * PASS * a, PACK * PASS * (a + 1))
             nc.scalar.copy(
-                out=rounded[:, cols].rearrange("p (t m j) -> p m t j", t=PACK, j=PACK),
-                in_=w2_raw[g][:, cols].rearrange("p (j m t) -> p m t j", j=PACK, t=PACK),
+                out=rounded[:, cols].rearrange("p (t m j) -> p m j t", t=PACK, j=PACK),
+                in_=w2_raw[g][:, cols].rearrange("p (j m t) -> p m j t", j=PACK, t=PACK),
             )
 
         def quantise_w2(g, rounded):

@@ -258,7 +258,11 @@ def tile_list_neutrino_tube_weave_kernel(
                         start=(a == 0), stop=(a == 1),
                     )
                 nc.scalar.activation(out=h2[s][:, cols], in_=bank[:], func=ACT.Exp, scale=-0.2)
-                nc.scalar.copy(out=bb[s][:, cols], in_=bank[:])
+                if s == SLICES - 1 and half == 0:
+                    nc.scalar.copy(out=b_late[:], in_=bank[:, 0:CHUNK])
+                    nc.scalar.copy(out=bb[s][:, CHUNK:BANK], in_=bank[:, CHUNK:BANK])
+                else:
+                    nc.scalar.copy(out=bb[s][:, cols], in_=bank[:])
 
         mid = [None] * SLICES
 
@@ -403,7 +407,6 @@ def tile_list_neutrino_tube_weave_kernel(
             scatter2(s - 1)
         filter2(6)
         decay2(6)
-        filter2(7)
         planes[0] = placed("planes0", [P, PACK, T2], BF16, at_b)
         accept(nc.gpsimd, 0, 0, T2)
         new_page(6)
@@ -412,10 +415,14 @@ def tile_list_neutrino_tube_weave_kernel(
         load_acc(3)
         load_acc(7)
         calibrate2(5, at_acc[0])
-        decay2(7)
-        load_acc(4)
+        b_late = placed("b_late", [P, CHUNK], F32, at_mid[1])
+        filter2(7)
         accept(nc.gpsimd, 2, 0, T2)
         load_acc(6, S - CHUNK)
+        mid[7] = rows[6][0][1][:, T2 - CHUNK : T2 - CHUNK + S]
+        late, early = slice(0, CHUNK), slice(CHUNK, S)
+        nc.gpsimd.tensor_tensor(out=mid[7][:, early], in0=h2[7][:, early], in1=bb[7][:, early], op=MULT)
+        load_acc(4)
         accept_halves(3)
         load_acc(5)
         calibrate2(6)
@@ -433,22 +440,15 @@ def tile_list_neutrino_tube_weave_kernel(
         new_page(7)
         scatter1(7)
         plane6 = placed("plane6", [P, T2], BF16, at_acc[5])
-        h2[7] = rows[6][0][1][:, T2 - CHUNK : T2 - CHUNK + S]
-        late, early = slice(0, CHUNK), slice(CHUNK, S)
-
-        def calibrate_last(cols):
-            nc.gpsimd.tensor_tensor(out=h2[7][:, cols], in0=mid[7][:, cols], in1=gain2[:, 3 * S : 4 * S][:, cols], op=MULT)
-
-        calibrate_last(early)
         accept(nc.gpsimd, 6, 0, T2, dst=plane6[:])
-        calibrate_last(late)
+        nc.gpsimd.tensor_tensor(out=mid[7][:, late], in0=h2[7][:, late], in1=b_late[:], op=MULT)
         z_w[0] = placed("z_w0", [P, T2], U32, at_b + 8)
         z_s[0] = placed("z_s0", [P, T2], U8, at_mid[1])
         quantise_z(0, 0, S)
         quantise_z(0, S, T2)
         for c in range(T2 // CHUNK):
             last_product(0, c)
-        scatter2(7)
+        nc.vector.tensor_tensor(pages[7][:].indirect(idx[3][:]), mid[7], gain2[:, 3 * S : 4 * S], MULT)
         half_pair(0, T2)
         woven[1] = placed("woven1", [P, PACK * T2], BF16, at_page[0])
         z_w[1] = placed("z_w1", [P, T2], U32, at_v)

from contextlib import ExitStack

import concourse.mybir as mybir

K, H, N, T, TC, S, T2 = 1024, 1024, 256, 4096, 2048, 1024, 2048
FLOPS = 2 * K * H * S * 2 + 2 * H * N * T2

F32 = mybir.dt.float32
BF16 = mybir.dt.bfloat16
I32 = mybir.dt.int32
U32 = mybir.dt.uint32
U16 = mybir.dt.uint16
U8 = mybir.dt.uint8
FP8X4 = mybir.dt.float8_e4m3fn_x4
FP4X4 = mybir.dt.float4_e2m1fn_x4
ACT = mybir.ActivationFunctionType
MULT = mybir.AluOpType.mult

P = 128
PACK = 4
PASS = P * PACK
BANK = 512
CHUNKS = T2 // BANK
SLICES = H // P
KIB = 1024
CHUNK = 256
ON_SCALAR = 5
LAG = 4


def tile_list_neutrino_tube_weave_kernel(
    tc, tab_words, tab_scales, tab2_words, tab2_scales, offs, offs2, offs3, offs4,
    w1_words, w1_scales, w2, w3_words, w3_scales, wg1, wg2, acc, out,
):
    nc = tc.nc
    with ExitStack() as ctx:
        lists = ctx.enter_context(tc.tile_pool(name="lists", bufs=1))
        shared = ctx.enter_context(tc.tile_pool(name="shared", bufs=1))
        psum = ctx.enter_context(tc.psum_pool(name="psum", bufs=1))

        def placed(name, shape, dtype, kib, shift=0, align=64):
            return shared.tile(shape, dtype, name=name, align_bytes=align, offset=kib * KIB + shift)

        idx = [lists.tile([P, S // 16], U16, name="idx%d" % i) for i in range(4)]
        banks = [psum.tile([P, BANK], F32, name="bank%d" % b) for b in range(8)]

        at_v2b, at_a, at_g, at_b, at_c, at_d = 0, 4, 20, 28, 60, 44
        at_page = [76, 92, 104, at_g, 84, 120, 76, at_b]
        at_x, at_y = 100, 116
        at_h1 = [136, 140, at_b + 4, at_b + 8, 144, 156, 152, 160]
        at_h2 = [at_a, at_a + 8, 128, 184, 144, 140, 176, 148]
        at_bb = [at_a + 4, at_a + 12, 132, 180, 164, 168, at_b, at_h1[0]]
        at_mid = [at_y, 172]
        at_acc = [at_c, at_c + 8, 222, at_c + 8, at_bb[2], at_c + 8, 222, at_page[1]]
        at_v, at_vs, at_v2, at_v2s = 188, 196, 198, 202
        at_v2, at_v2b = at_v2b, at_v2
        at_w1, at_w1s, at_w1sr, at_w2, at_w2s, at_w3s, at_w2b = 203, 207, 209, 211, 215, 217, 218

        seed = placed("seed", [P, 2 * SLICES], F32, at_w3s, shift=640)[:]
        tab_w = [placed("tab_w%d" % a, [P, T], I32, (at_g, at_a)[a]) for a in range(2)]
        w1_raw = placed("w1_raw", [P, 2, H // 2], I32, at_a + 4)[:]
        tab2_w = [placed("tab2_w0", [P, TC], I32, at_g + 16), placed("tab2_w1", [P, TC], I32, at_d)]
        tab_s = placed("tab_s", [P, T], U8, at_a)
        picked = [placed("picked%d" % i, [P, S], U8, 230 + i) for i in range(2)]
        tab2_s = placed("tab2_s", [P, TC], U8, at_bb[2])
        w1_s_raw = placed("w1_s_raw", [P, 56 * KIB], U8, at_d - 1)[:, 0 : 2 * H].rearrange("p (a c) -> p a c", a=2)
        w1_w = [placed("w1_w%d" % g, [P, 2, H], U8, at_w1 + 2 * g) for g in range(2)]
        w1_s = [placed("w1_s%d" % g, [P, 2, PASS], U8, (at_w1s, at_acc[2])[g]) for g in range(2)]
        zero = placed("zero", [P, 2 * SLICES], F32, at_w3s, shift=512)
        v_w = [placed("v_w0", [P, S], U32, at_v), None]
        v2_w = [placed("v2_w0", [P, S], U32, at_v2)]
        v_s = [placed("v_s%d" % a, [P, S], U8, at_vs + a) for a in range(2)]
        v2_s = placed("v2_s", [P, S], U8, at_v2s)
        w2_s = [placed("w2_s%d" % g, [P, 2 * PASS], U8, at_w2s + g) for g in range(2)]
        w2_w = [placed("w2_w0", [P, 2 * PASS], U32, at_w2), None]
        one = placed("one", [P, 1], F32, at_w3s, shift=768)[:]

        nc.vector.memset(w1_s_raw.rearrange("p a c -> p (a c)").bitcast(I32), 0)
        nc.vector.memset(seed, 1.0)
        nc.scalar.activation(out=zero[:], in_=seed, func=ACT.Ln)
        nc.vector.memset(tab_s[64:P, :].bitcast(I32), 0)
        nc.gpsimd.memset(tab_s[32:64, :].bitcast(I32), 0)
        nc.vector.memset(tab2_s[0:64, :].bitcast(I32), 0)
        nc.gpsimd.memset(tab2_s[96:P, :].bitcast(I32), 0)
        for cleared in (v_s[0][:], v_s[1][:], v2_s[:]):
            nc.gpsimd.memset(cleared.bitcast(I32), 0)
        nc.vector.memset(one, 1.0)

        def load_packed_scales(queue, dst, scales):
            for quad in range(4):
                queue.dma_start(
                    out=dst[32 * quad : 32 * quad + 8, :].bitcast(I32),
                    in_=scales[:, 4 * quad : 4 * quad + 4, :].bitcast(I32),
                )

        def load_rows(dst, scales):
            nc.sync.dma_start(out=dst.bitcast(I32), in_=scales.bitcast(I32).rearrange("a q t -> (a q) t"))

        def deal(queues, dst, first, src, a):
            for r in range(4):
                queues[r].dma_start(
                    out=dst[first + r : P : 32, :].bitcast(I32),
                    in_=src[16 * a + r : 16 * (a + 1) : 4, :].bitcast(I32),
                )

        def words(src):
            return src.rearrange("p t i -> p (t i)").bitcast(I32)

        def load_gain(dst, wg, c0, c1):
            view = wg.rearrange("(m t) j -> m (t j)", t=PACK)
            for quad in (0, 2, 1, 3):
                nc.sync.dma_start(out=dst[32 * quad : 32 * quad + 32, c0:c1], in_=view[:, c0:c1])

        nc.sync.dma_start(idx[0][:], offs)
        load_rows(tab_s[0:32, :], tab_scales)
        nc.sync.dma_start(out=w1_raw, in_=w1_words.bitcast(I32).rearrange("a p c -> p a c"))
        for r in range(4):
            nc.sync.dma_start(
                out=w1_s_raw[r:P:32, :, :].bitcast(I32),
                in_=w1_scales[:, r:16:4, :].bitcast(I32).rearrange("a q c -> q a c"),
            )
        nc.sync.dma_start(out=tab_w[0][:], in_=words(tab_words[0]))
        nc.sync.dma_start(idx[1][:], offs2)
        load_rows(tab2_s[64:96, :], tab2_scales)

        def load_w2(g):
            dst = placed("w2_raw%d" % g, [P, 2 * PACK * PASS], F32, (at_x - 2, at_a)[g], shift=64 * g)
            for a in range(2):
                nc.sync.dma_start(
                    out=dst[:, PACK * PASS * a : PACK * PASS * (a + 1)].rearrange("p (j c) -> p j c", j=PACK),
                    in_=w2[PASS * a : PASS * (a + 1), PASS * g : PASS * (g + 1)].rearrange("(p j) c -> p j c", j=PACK),
                )
            return dst

        rows = [[] for s in range(SLICES)]

        def acc_rows(s):
            g, t = divmod(s, PACK)
            return acc[PASS * g : PASS * (g + 1), :].rearrange("(p t) m -> t p m", t=PACK)[t]

        def load_acc(s, spare=0):
            whole = placed("acc%d" % s, [P, T2 + spare], F32, at_acc[s])
            nc.sync.dma_start(out=whole[:, 0:T2], in_=acc_rows(s))
            rows[s].append((0, whole))

        def load_acc_half(s, half, kib):
            part = placed("acc%d_%d" % (s, half), [P, S], F32, kib)
            nc.sync.dma_start(out=part[:], in_=acc_rows(s)[:, S * half : S * (half + 1)])
            rows[s].append((S * half, part))

        nc.vector.tensor_copy(picked[0][:], tab_s[:].indirect(idx[0][:]))
        for a in range(2):
            deal([nc.scalar if 4 * a + r < 3 else nc.gpsimd for r in range(4)], v_s[a], 0, picked[0], a)
        for g in range(2):
            nc.vector.tensor_copy(
                out=w1_w[g][:].bitcast(U16).rearrange("p a (t m) -> p a t m", t=PACK),
                in_=w1_raw[:, :, PASS // 2 * g : PASS // 2 * (g + 1)].bitcast(U16).rearrange("p a (m t) -> p a t m", t=PACK),
            )
        for g in range(2):
            nc.vector.tensor_copy(
                out=w1_s[g][:].rearrange("p a (t m) -> p a t m", t=PACK),
                in_=w1_s_raw[:, :, PASS * g : PASS * (g + 1)].rearrange("p a (m t) -> p a t m", t=PACK),
            )
        nc.sync.dma_start(out=tab_w[1][:], in_=words(tab_words[1]))
        gain1 = placed("gain1", [P, PACK * S], F32, at_c)
        nc.sync.dma_start(out=tab2_w[0][:], in_=words(tab2_words[0]))
        nc.sync.dma_start(out=tab2_w[1][:], in_=words(tab2_words[1]))
        load_gain(gain1, wg1, 0, BANK)
        nc.sync.dma_start(idx[2][:], offs3)
        load_gain(gain1, wg1, BANK, S)
        nc.sync.dma_start(idx[3][:], offs4)
        nc.vector.tensor_copy(v_w[0][:], tab_w[0][:].bitcast(U32).indirect(idx[0][:]))
        nc.vector.tensor_copy(picked[1][:], tab2_s[:].indirect(idx[1][:]))
        v_w[1] = placed("v_w1", [P, S], U32, at_v + 4)
        for half in range(2):
            nc.vector.tensor_copy(
                v_w[1][:, BANK * half : BANK * (half + 1)],
                tab_w[1][:].bitcast(U32).indirect(idx[0][:, BANK // 16 * half : BANK // 16 * (half + 1)]),
            )

        nc.vector.tensor_copy(v2_w[0][:], tab2_w[0][:].bitcast(U32).indirect(idx[1][:]))
        v2_w.append(placed("v2_w1", [P, S], U32, at_v2b))
        nc.vector.tensor_copy(v2_w[1][:], tab2_w[1][:].bitcast(U32).indirect(idx[1][:]))
        w2_raw = [load_w2(0), None]
        for t in range(1, PACK):
            load_gain(gain1, wg1, t * S, (t + 1) * S)
        gain2 = placed("gain2", [P, PACK * S], F32, at_d)
        load_gain(gain2, wg2, 0, S)
        w2_raw[1] = load_w2(1)
        for a in range(2):
            deal([nc.sync] * 4, v2_s, 4 * a, picked[1][64:96, :], a)
        load_gain(gain2, wg2, S, PACK * S)

        def round_w2(g, a, rounded):
            cols = slice(PACK * PASS * a, PACK * PASS * (a + 1))
            nc.scalar.copy(
                out=rounded[:, cols].rearrange("p (t m j) -> p m j t", t=PACK, j=PACK),
                in_=w2_raw[g][:, cols].rearrange("p (j m t) -> p m j t", j=PACK, t=PACK),
            )

        def quantise_w2(g, rounded):
            nc.vector.quantize_mx(out=w2_w[g][:].bitcast(FP8X4), scales=w2_s[g][:], in_=rounded[:])

        halves = (slice(0, BANK), slice(BANK, S))
        bank_pairs = [banks[0:2], banks[2:4]]
        h1 = [None] * SLICES
        h2 = [None] * SLICES
        bb = [None] * SLICES
        pages = [None] * SLICES

        def square1(s, half, dst):
            g, t = divmod(s, PACK)
            bank = bank_pairs[1 - g][half]
            cols = halves[half]
            for a in range(2):
                nc.tensor.matmul_mx(
                    out=bank[:],
                    lhsT=w1_w[g][:, a, 2 * P * t : 2 * P * (t + 1)].bitcast(FP4X4),
                    lhsT_scale=w1_s[g][:, a, P * t : P * (t + 1)],
                    rhs=v_w[a][:, cols].bitcast(FP8X4),
                    rhs_scale=v_s[a][:, cols],
                    start=(a == 0), stop=(a == 1),
                )
            column = 2 * s + half
            nc.scalar.activation(out=dst, in_=bank[:], func=ACT.Square, bias=zero[:, column : column + 1])

        def log1p(dst, src):
            nc.scalar.activation(out=dst, in_=src, func=ACT.Ln, bias=one)

        def filter1(s, raw, log):
            for half, cols in enumerate(halves):
                square1(s, half, raw[:, cols])
            log1p(log[:], raw[:])

        def calibrate1(s, dst, raw, cols=slice(0, S)):
            t = s % PACK
            nc.gpsimd.tensor_tensor(out=dst, in0=raw, in1=gain1[:, t * S : (t + 1) * S][:, cols], op=MULT)

        def make_h1(s):
            h1[s] = placed("h1_%d" % s, [P, S], F32, at_h1[s])
            filter1(s, h1[s], h1[s])
            calibrate1(s, h1[s][:], h1[s][:])

        def filter2(s):
            g, t = divmod(s, PACK)
            h2[s] = placed("h2_%d" % s, [P, S], F32, at_h2[s])
            bb[s] = placed("b_%d" % s, [P, S], F32, at_bb[s])
            for half, bank in enumerate(bank_pairs[(s + 1) % 2]):
                cols = slice(BANK * half, BANK * (half + 1))
                for a in range(2):
                    stationary = slice(PASS * a + P * t, PASS * a + P * (t + 1))
                    nc.tensor.matmul_mx(
                        out=bank[:],
                        lhsT=w2_w[g][:, stationary].bitcast(FP8X4),
                        lhsT_scale=w2_s[g][:, stationary],
                        rhs=v2_w[a][:, cols].bitcast(FP8X4),
                        rhs_scale=v2_s[4 * a : P, cols],
                        start=(a == 0), stop=(a == 1),
                    )
                nc.scalar.activation(out=h2[s][:, cols], in_=bank[:], func=ACT.Exp, scale=-0.2)
                if s == SLICES - 1 and half == 0:
                    nc.scalar.copy(out=b_late[:], in_=bank[:, 0:CHUNK])
                    nc.scalar.copy(out=bb[s][:, CHUNK:BANK], in_=bank[:, CHUNK:BANK])
                else:
                    nc.scalar.copy(out=bb[s][:, cols], in_=bank[:])

        mid = [None] * SLICES

        def decay2(s):
            mid[s] = placed("mid%d" % s, [P, S], F32, at_mid[s % 2])
            nc.gpsimd.tensor_tensor(out=mid[s][:], in0=h2[s][:], in1=bb[s][:], op=MULT)

        def calibrate2(s, kib=None):
            t = s % PACK
            h2[s] = placed("h2_done%d" % s, [P, S], F32, at_h2[s] if kib is None else kib)
            nc.gpsimd.tensor_tensor(out=h2[s][:], in0=mid[s][:], in1=gain2[:, t * S : (t + 1) * S], op=MULT)

        def new_page(s):
            pages[s] = placed("page%d" % s, [P, T2], F32, at_page[s])

        def scatter1(s):
            nc.vector.tensor_copy(pages[s][:].indirect(idx[2][:]), h1[s][:])

        def scatter2(s):
            nc.vector.tensor_copy(pages[s][:].indirect(idx[3][:]), h2[s][:])

        planes = [None, None]
        woven = [None, None]

        def accept(engine, s, m0, m1, dst=None):
            first, part = [(at, part) for at, part in rows[s] if at <= m0][-1]
            engine.tensor_tensor(
                out=planes[s // PACK][:, s % PACK, m0:m1] if dst is None else dst,
                in0=pages[s][:, m0:m1],
                in1=part[:, m0 - first : m1 - first],
                op=MULT,
            )

        def accept_halves(s):
            accept(nc.gpsimd, s, 0, S)
            accept(nc.gpsimd, s, S, T2)

        def weave(copy, g, m0, m1):
            copy(
                out=woven[g][:, PACK * m0 : PACK * m1].rearrange("p (u i t) -> p u t i", i=4, t=PACK),
                in_=planes[g][:, :, m0:m1].rearrange("p t (u i) -> p u t i", i=4),
            )

        def pair_up(m0, m1):
            nc.scalar.copy(
                out=pairs[:, 0, m0:m1, :].rearrange("p (u i) t -> p u t i", i=8),
                in_=planes[1][:, 0:2, m0:m1].rearrange("p t (u i) -> p u t i", i=8),
            )

        def half_pair(m0, m1):
            nc.scalar.copy(
                out=pairs[:, 1, m0:m1, :],
                in_=plane6[:, m0:m1].unsqueeze(2).to_broadcast([P, m1 - m0, 2]),
            )

        def weave_pairs(copy, word, m0, m1):
            copy(
                out=woven[1][:, PACK * m0 : PACK * m1].bitcast(word).rearrange("p (u i h) -> p u h i", i=4, h=2),
                in_=pairs[:].rearrange("p h m t -> p h (m t)").bitcast(word)[:, :, m0:m1].rearrange("p h (u i) -> p u h i", i=4),
            )

        z_w = [None, None]
        z_s = [None, None]

        def quantise_z(g, m0, m1):
            nc.vector.quantize_mx(
                out=z_w[g][:, m0:m1].bitcast(FP8X4), scales=z_s[g][:, m0:m1], in_=woven[g][:, PACK * m0 : PACK * m1]
            )

        def last_product(g, c):
            cols = slice(CHUNK * c, CHUNK * (c + 1))
            for n in range(N // P):
                nc.tensor.matmul_mx(
                    out=banks[c][:, CHUNK * n : CHUNK * (n + 1)],
                    lhsT=w3_w[:, g, P * n : P * (n + 1)].bitcast(FP8X4),
                    lhsT_scale=w3_s[4 * g : P, P * n : P * (n + 1)],
                    rhs=z_w[g][:, cols].bitcast(FP8X4),
                    rhs_scale=z_s[g][:, cols],
                    start=(g == 0 and n == 0), stop=(g == 1 and n == N // P - 1),
                )

        def store(c, copy, queue):
            stage = placed("stage%d" % c, [P, BANK], F32, at_d + 2 * c)
            copy(out=stage[:], in_=banks[c][:])
            queue.dma_start(
                out=out.rearrange("(n p) m -> p n m", p=P)[:, :, CHUNK * c : CHUNK * (c + 1)],
                in_=stage[:].rearrange("p (n m) -> p n m", m=CHUNK),
            )

        new_page(0)
        new_page(4)
        for (s, half), at_square in zip(((0, 0), (4, 0), (0, 1), (4, 1)), (1, 0, 2, 0)):
            square = placed("square%d%d" % (s, half), [P, BANK], F32, at_h1[1] + at_square)[:]
            part = placed("h1_%d%d" % (s, half), [P, BANK], F32, at_h1[s] + 2 * half)[:]
            square1(s, half, square)
            log1p(part, square)
            calibrate1(s, part, part, halves[half])
            offsets = idx[2][:, BANK // 16 * half : BANK // 16 * (half + 1)]
            nc.vector.tensor_copy(pages[s][:].indirect(offsets), part)
        make_h1(1)
        h1[5] = placed("h1_5", [P, S], F32, at_h1[5])
        filter1(5, placed("raw5", [P, S], F32, at_b), h1[5])
        calibrate1(5, h1[5][:], h1[5][:])
        rounded = placed("w2_bf16_0", [P, 2 * PACK * PASS], BF16, at_b)
        round_w2(0, 0, rounded)
        round_w2(0, 1, rounded)
        quantise_w2(0, rounded)
        for s in (2, 6):
            raw = placed("raw%d" % s, [P, S], F32, at_x + 3 * (s - 2))
            h1[s] = placed("h1_%d" % s, [P, S], F32, at_h1[s])
            filter1(s, raw, raw)
            calibrate1(s, h1[s][:], raw[:])
        make_h1(3)
        raw7 = placed("raw7", [P, S], F32, at_y)
        h1[7] = placed("h1_7", [P, S], F32, at_h1[7])
        filter1(7, raw7, h1[7])
        calibrate1(7, h1[7][:], h1[7][:])
        w3_s = w1_s[0][:, 0, 0:N]
        load_packed_scales(nc.sync, w3_s, w3_scales)
        w3_w = placed("w3_w", [P, 2, N], I32, at_w1)
        nc.sync.dma_start(out=w3_w[:], in_=w3_words.rearrange("a p c i -> p a (c i)").bitcast(I32))
        for s in (1, 2):
            new_page(s)
            scatter1(s)
        rounded = placed("w2_bf16_1", [P, 2 * PACK * PASS], BF16, at_y - 2)
        round_w2(1, 0, rounded)
        round_w2(1, 1, rounded)
        w2_w[1] = placed("w2_w1", [P, 2 * PASS], U32, at_w2b)
        quantise_w2(1, rounded)
        for s in (3, 5):
            new_page(s)
            scatter1(s)
        load_acc(0)
        load_acc(1)
        load_acc(2)
        filter2(0)
        decay2(0)
        for s in range(1, 6):
            filter2(s)
            decay2(s)
            calibrate2(s - 1)
            scatter2(s - 1)
        filter2(6)
        decay2(6)
        planes[0] = placed("planes0", [P, PACK, T2], BF16, at_b)
        accept(nc.gpsimd, 0, 0, T2)
        new_page(6)
        scatter1(6)
        accept(nc.gpsimd, 1, 0, T2)
        load_acc(3)
        load_acc(7)
        calibrate2(5, at_acc[0])
        b_late = placed("b_late", [P, CHUNK], F32, at_mid[1])
        filter2(7)
        accept(nc.gpsimd, 2, 0, T2)
        load_acc(6, S - CHUNK)
        mid[7] = rows[6][0][1][:, T2 - CHUNK : T2 - CHUNK + S]
        late, early = slice(0, CHUNK), slice(CHUNK, S)
        nc.gpsimd.tensor_tensor(out=mid[7][:, early], in0=h2[7][:, early], in1=bb[7][:, early], op=MULT)
        load_acc(4)
        accept_halves(3)
        load_acc(5)
        calibrate2(6)
        woven[0] = placed("woven0", [P, PACK * T2], BF16, at_a)
        for m in range(0, T2, BANK):
            weave(nc.scalar.copy, 0, m, m + BANK)
        for s in (5, 6):
            scatter2(s)
        planes[1] = placed("planes1", [P, 2, T2], BF16, at_h1[1])
        pairs = placed("pairs", [P, 2, T2, 2], BF16, at_x)
        accept(nc.gpsimd, 4, 0, T2)
        accept(nc.gpsimd, 5, 0, T2)
        pair_up(0, S)
        pair_up(S, T2)
        new_page(7)
        scatter1(7)
        plane6 = placed("plane6", [P, T2], BF16, at_acc[5])
        accept(nc.gpsimd, 6, 0, T2, dst=plane6[:])
        nc.gpsimd.tensor_tensor(out=mid[7][:, late], in0=h2[7][:, late], in1=b_late[:], op=MULT)
        z_w[0] = placed("z_w0", [P, T2], U32, at_b + 8)
        z_s[0] = placed("z_s0", [P, T2], U8, at_mid[1])
        quantise_z(0, 0, S)
        quantise_z(0, S, T2)
        for c in range(T2 // CHUNK):
            last_product(0, c)
        nc.vector.tensor_tensor(pages[7][:].indirect(idx[3][:]), mid[7], gain2[:, 3 * S : 4 * S], MULT)
        half_pair(0, T2)
        woven[1] = placed("woven1", [P, PACK * T2], BF16, at_page[0])
        z_w[1] = placed("z_w1", [P, T2], U32, at_v)
        z_s[1] = placed("z_s1", [P, T2], U8, at_vs)

        def accept_last(c0, c1):
            accept(nc.vector, SLICES - 1, CHUNK * c0, CHUNK * c1, dst=pairs[:, 1, CHUNK * c0 : CHUNK * c1, 1])

        def weave_last(on_scalar, c):
            copy, word = (nc.scalar.copy, U32) if on_scalar else (nc.vector.tensor_copy, I32)
            weave_pairs(copy, word, CHUNK * c, CHUNK * (c + 1))

        def finish(c):
            quantise_z(1, CHUNK * c, CHUNK * (c + 1))
            last_product(1, c)

        last = T2 // CHUNK
        for c in range(last):
            accept_last(c, c + 1)
            if c < ON_SCALAR:
                weave_last(True, c)
            if c >= LAG:
                finish(c - LAG)
        for c in range(last - LAG, last):
            if ON_SCALAR <= c + 1 < last:
                weave_last(False, c + 1)
            finish(c)
        for c in range(last - 1):
            store(c, nc.scalar.copy, nc.sync)
        store(last - 1, nc.scalar.copy, nc.sync)
